import numpy as np, ml_dtypes
CORES = [1,5,17,21,33,37,49,53]
N = 8
import mx_ref
BF = ml_dtypes.bfloat16
def entries(a):
    return np.ascontiguousarray(a.T).reshape(-1)
def table(e):
    return np.ascontiguousarray(np.reshape(e, (-1, 16)).T).astype(np.int32)
def cut(t, i, w=512):
    return t[:, w * i:w * i + w]
def f(rng, *shape):
    return mx_ref.flush((rng.standard_normal(shape, dtype=np.float32) * np.exp2(rng.integers(-2, 3, shape[:-1] + (1,)))).astype(BF))
def wide(rng, *shape, cols=0):
    v = rng.standard_normal(shape, dtype=np.float32) * np.exp2(rng.integers(-12, 13, shape)).astype(np.float32)
    if cols: v *= np.repeat(np.exp2(rng.integers(-cols, cols + 1, shape[:-2] + (1, shape[-1] // 4))) * (rng.random(shape[:-2] + (1, shape[-1] // 4)) > 0.0625), 4, axis=-1).astype(np.float32)
    return mx_ref.flush(v.astype(BF))
PG, NW, SP, CW, CP, O = 32, 64, 32, 16, 6, 2
def counts(rng, total, cap, least):
    n = np.array(least)
    while n.sum() < total: n[rng.choice(np.flatnonzero(n < cap))] += 1
    return n
def lists(rng, full=False, own=False, shared=False, rewritten=False):
    h = int(rng.integers(0, N)); hot = rng.permutation(PG)[:CP if shared else 2]
    fr, pg = np.zeros((N, SP), int), np.zeros((N, SP), int)
    rd, wr, wp = np.full((N, N * CP), -1), np.full((N, N * CW), -1), np.full((N, N * CW), -1)
    for s in range(N):
        lw, lp = np.zeros(N, int), np.zeros(N, int)
        if full:
            a = np.append(h, rng.permutation(np.delete(np.arange(N), h)))
            lw[a[:NW // CW]] = CW; lp[a[:SP // CP]] = CP
        if own: lw[s] = CW; lp[s] = CP
        if shared: lw[h] = CW; lp[h] = CP
        if rewritten: lw[h] = CW; lp[h] = 1
        n, fresh, at = counts(rng, NW, CW, lw), rng.permutation(NW), 0
        for q in range(N):
            c = rng.permutation(CW)[:n[q]]
            wr[s, q * CW + c] = fresh[at:at + n[q]]; wp[q, s * CW + c] = 0; at += n[q]
        n, slots, frames = counts(rng, SP, CP, lp), [], []
        for q in range(N):
            must = np.zeros(0, int)
            if q == h and shared: must = hot
            if q == h and rewritten: must = hot[s % 2:s % 2 + 1]
            g = np.concatenate([must, rng.permutation(np.setdiff1d(np.arange(PG), must))])[:n[q]]
            c = rng.permutation(CP)[:n[q]]
            rd[q, s * CP + c] = g; slots.append(q * CP + c); frames.append(q * PG + g)
        o = rng.permutation(SP)
        pg[s] = np.concatenate(slots)[o]; fr[s] = np.concatenate(frames)[o]
    for q in range(N):
        k = np.flatnonzero(wp[q] >= 0); must = np.zeros(0, int)
        if q == h and shared: must = 16 * hot + rng.integers(0, 16, hot.size)
        if q == h and rewritten: must = (16 * hot[:, None] + np.arange(16)).reshape(-1)
        p = np.concatenate([must, rng.permutation(np.setdiff1d(np.arange(16 * PG), must))])[:k.size]
        wp[q, k] = rng.permutation(p)
    return {n: np.stack([table(v) for v in a]) for n, a in (("fr", fr), ("wr", wr), ("wp", wp), ("rd", rd), ("pg", pg))}
def setup_inputs(rng):
    return {"pl": f(rng, N, 128, 64 * PG), "nw": f(rng, N, 128, 4 * NW), "qw": f(rng, N, 128, 512 * O), **lists(rng)}
def setup_inputs_full(rng):
    return {**setup_inputs(rng), **lists(rng, full=True)}
def setup_inputs_own(rng):
    return {**setup_inputs(rng), **lists(rng, own=True)}
def setup_inputs_rewritten(rng):
    return {**setup_inputs(rng), **lists(rng, rewritten=True)}
def setup_inputs_shared(rng):
    return {**setup_inputs(rng), **lists(rng, shared=True)}
def setup_inputs_spread(rng):
    d = setup_inputs(rng); d["pl"] = wide(rng, N, 128, 64 * PG, cols=8); d["nw"] = wide(rng, N, 128, 4 * NW, cols=8); return d
def check_inputs(d):
    b = []
    for r in range(N):
        t, a, p, k, g = [entries(d[n][r]) for n in ("fr", "wr", "wp", "rd", "pg")]
        if t.min() < 0 or t.max() >= N * PG or len(set(t.tolist())) != SP: b.append("fr")
        if a.min() < -1 or a.max() >= NW or sorted(a[a >= 0].tolist()) != list(range(NW)): b.append("wr")
        sent = np.concatenate([entries(d["wr"][s])[r * CW:r * CW + CW] for s in range(N)]); v = p[p >= 0]
        if p.min() < -1 or p.max() >= 16 * PG or len(set(v.tolist())) != v.size or ((p >= 0) != (sent >= 0)).any(): b.append("wp")
        if k.min() < -1 or k.max() >= PG: b.append("rd")
        got = np.concatenate([entries(d["rd"][q])[r * CP:r * CP + CP] for q in range(N)])
        if g.min() < 0 or g.max() >= N * CP or len(set(g.tolist())) != SP or (got >= 0).sum() != SP: b.append("pg")
        elif (got[g] < 0).any() or (g // CP * PG + got[g] != t).any(): b.append("pg")
    return b
def reference(pl, nw, qw, fr, wr, wp, rd, pg):
    pools = []
    for q in range(N):
        v = pl[q].reshape(128, 16 * PG, 4).copy()
        for s in range(N):
            c, p = entries(wr[s])[q * CW:q * CW + CW], entries(wp[q])[s * CW:s * CW + CW]
            k = p >= 0
            v[:, p[k]] = nw[s].reshape(128, NW, 4)[:, c[k]]
        pools.append(v)
    pools = np.concatenate(pools, axis=1)
    y = np.zeros((N, 128, O * SP * 16), np.float32)
    for r in range(N):
        e = (16 * entries(fr[r])[:, None] + np.arange(16)).reshape(-1)
        pages = mx_ref.quantize(np.ascontiguousarray(pools[:, e]).reshape(128, -1))
        for o in range(O):
            y[r][:, SP * 16 * o:SP * 16 * o + SP * 16] = mx_ref.matmul(mx_ref.quantize(np.ascontiguousarray(cut(qw[r], o))), pages)
    return {"y": y}

@@ -1,0 +1,254 @@
+from concourse.bass import DstId, RemoteDMATransfer
+from concourse.mybir import dt, AluOpType, ActivationFunctionType
+
+N = 8
+PG, NW, SP, CW, CP, O = 32, 64, 32, 16, 6, 2
+POOL = 16 * PG
+WIN = POOL + N * CW
+PC = 16 * CP
+ROW = POOL + 32
+DUMP = ROW - 16
+SROW = 800
+CH = 4
+CC = 16 * SP // CH
+
+F8, U8, U16, I32, F32, BF = "float8_e4m3fn_x4", "uint8", "uint16", "int32", "float32", "bfloat16"
+
+
+def _sb(n, d):
+    return ("sbuf", [128, n], d)
+
+
+SCRATCH = {
+    "nwt": _sb(512, BF), "plt": _sb(4 * POOL, BF), "qwt": _sb(512 * O, BF),
+    "lwr": _sb(8, I32), "lwp": _sb(8, I32), "lrd": _sb(4, I32), "lpg": _sb(2, I32),
+    "pcol": _sb(1, I32), "pand": _sb(2, I32), "cold": _sb(1, F32), "coln": _sb(1, F32), "colg": _sb(1, F32),
+    "ck": _sb(8, I32), "cnt": _sb(WIN, F32), "cslot": _sb(48, F32), "wslot": _sb(48, F32),
+    "offa": _sb(8, U16), "offo": _sb(2, U16), "offw": _sb(8, U16), "offr": _sb(4, U16), "offb": _sb(48, U16),
+    "offg": _sb(2, U16), "offc": _sb(32, U16),
+    "w1": _sb(8, I32), "w2": _sb(8, F32), "r1": _sb(4, F32),
+    "srow": _sb(SROW, F32), "srct": _sb(ROW, F32),
+    "nwq": _sb(128, F8), "nws": _sb(128, U8),
+    "sndw": _sb(N * CW, F8), "sndws": _sb(N * CW, U8),
+    "win": _sb(WIN, F8), "wins": _sb(WIN, U8),
+    "sndp": _sb(N * PC, F8), "sndps": _sb(N * PC, U8),
+    "land": _sb(N * PC, F8), "lands": _sb(N * PC, U8),
+    "fin": _sb(16 * SP, F8), "fins": _sb(16 * SP, U8),
+    "qwq": _sb(128 * O, F8), "qws": _sb(128 * O, U8),
+    "ps": ("psum", [128, 512 * CH * O], F32),
+    "yb": _sb(512 * O, F32),
+}
+SEMAPHORES = (["dnw", "dwr", "dwp", "drd", "dpg", "dpl", "dqw", "ystore"]
+              + ["i_p", "i_k", "i_c", "i_s", "cn", "row"]
+              + ["v%d" % k for k in range(24)]
+              + ["nq", "oa", "oo", "oc", "ob", "plq", "qwd",
+                 "pka", "pkas", "owna", "ownas",
+                 "ownb", "ownbs"]
+              + ["pkb%d" % k for k in range(4)] + ["pkbs%d" % k for k in range(4)]
+              + ["fc%d" % k for k in range(CH)] + ["fs%d" % k for k in range(CH)]
+              + ["mm%d" % k for k in range(CH * O)] + ["cp%d" % k for k in range(CH * O)]
+              + ["arwc", "arws", "arpc", "arps", "left"])
+
+
+def _chips(T, topo):
+    chips = {}
+    for r, c in enumerate(T.cores):
+        chips.setdefault(topo.chip(c), []).append(r)
+    return [chips[k] for k in sorted(chips)]
+
+
+def _roads(T, topo, r):
+    chips = _chips(T, topo)
+    at = [k for k, m in enumerate(chips) if r in m][0]
+    away = [chips[(at + k) % len(chips)] for k in range(1, len(chips))]
+    near = [q for q in chips[at] if q != r]
+    out = topo.engines(T.cores[r], T.cores[away[0][0]])
+    inn = [e for e in topo.engines(T.cores[r], T.cores[near[0]]) if e not in out]
+    return away, near, out, inn
+
+
+def _deal(dests, engines):
+    k = len(engines) // len(dests)
+    return [(d, engines[k * i:k * i + k]) for i, d in enumerate(dests)]
+
+
+def _plan(T, topo, r, phase):
+    away, near, out, inn = _roads(T, topo, r)
+    if phase == "A":
+        return [_deal(away[0] + away[1], out) + _deal(near, inn[:2]), _deal(away[2], out)]
+    return [_deal(away[0], out), _deal(away[1] + away[2], out) + _deal(near, inn[:2])]
+
+
+def rank_program(g, core, T, topo):
+    me = T.rank_of(core)
+    if me is None:
+        return
+    S = T.sem
+    V, A, P, Y = g.vector, g.scalar, g.tensor, g.sync
+    Op, Copy = AluOpType, ActivationFunctionType.Copy
+    nv = [0]
+
+    def wait(q, *evs):
+        for e in evs:
+            n, k = e if isinstance(e, tuple) else (e, 1)
+            q.wait_ge(S[n], k)
+
+    def step(call):
+        n = "v%d" % nv[0]
+        nv[0] += 1
+        call.then_inc(S[n], 1)
+        return n
+
+    arrive = {}
+    for ph in "AB":
+        arrive[ph] = sum(len(e) for r in range(N) if r != me for call in _plan(T, topo, r, ph) for d, e in call if d == me)
+
+    def table(q, dst, src, cols, sem, groups):
+        for k in groups:
+            q.dma_start(dst[16 * k:16 * k + 16, 0:cols], src[:, :]).then_inc(S[sem], 16)
+
+    table(A, T.lwr, T.wr, 8, "dwr", range(0, 4))
+    A.dma_start(T.qwt[:, :], T.qw[:, :]).then_inc(S.dqw, 16)
+    Y.dma_start(T.nwt[:, 0:4 * NW], T.nw[:, :]).then_inc(S.dnw, 16)
+    table(Y, T.lwr, T.wr, 8, "dwr", range(4, 8))
+    Y.dma_start(T.plt[:, :], T.pl[:, :]).then_inc(S.dpl, 16)
+    table(Y, T.lwp, T.wp, 8, "dwp", range(8))
+    table(Y, T.lrd, T.rd, 3, "drd", range(8))
+    table(Y, T.lpg, T.pg, 2, "dpg", range(8))
+
+    g.iota(T.pcol[:, :], [[1, 1]], 0, 1).then_inc(S.i_p, 1)
+    g.iota(T.ck[:, :], [[16, 8]], DUMP, 1).then_inc(S.i_k, 1)
+    g.iota(T.cnt[:, :], [[1, WIN]], 0, 0, allow_small_or_imprecise_dtypes=True).then_inc(S.i_c, 1)
+
+    z = step(V.memset(T.nwt[:, 4 * NW:512], 0.0))
+    wait(V, "i_p")
+    a1 = step(V.tensor_scalar(T.pand[:, 0:1], T.pcol[:, 0:1], 16, None, Op.bitwise_and))
+    wait(V, a1)
+    V.tensor_scalar(T.coln[:, :], T.pand[:, 0:1], 32.0, None, Op.subtract).then_inc(S.cn, 1)
+    a2 = step(V.tensor_scalar(T.cold[:, :], T.pand[:, 0:1], -1.0, 32.0, Op.mult, Op.add))
+
+    wait(V, ("dwr", 128))
+    V.tensor_copy(T.offa[:, :], T.lwr[:, :]).then_inc(S.oa, 1)
+    wait(V, z, ("dnw", 16))
+    V.quantize_mx(T.nwq[:, :], T.nws[:, :], T.nwt[:, :]).then_inc(S.nq, 1)
+    wait(V, "oa", "nq")
+    V.tensor_copy(T.sndw[:, :].bitcast(dt.uint32), T.nwq[:, 0:NW].bitcast(dt.uint32).indirect(T.offa[:, 0:8])).then_inc(S.pka, 1)
+    V.tensor_copy(T.offo[:, 0:1], T.lwr[:, me:me + 1]).then_inc(S.oo, 1)
+    own = POOL + CW * me
+
+    wait(A, "oa", "nq")
+    A.activation(T.sndws[:, :], T.nws[:, 0:NW].indirect(T.offa[:, 0:8]), Copy).then_inc(S.pkas, 1)
+    wait(A, "i_c", "cn")
+    A.activation(T.srow[:, 0:ROW], T.cnt[:, 0:ROW], ActivationFunctionType.Identity, bias=T.coln[:, 0:1]).then_inc(S.row, 1)
+    wait(A, "oo")
+    A.activation(T.wins[:, own:own + CW], T.nws[:, 0:NW].indirect(T.offo[:, 0:1]), Copy).then_inc(S.ownas, 1)
+
+    left = [0]
+
+    def send(call, src, dst, w, to, codes, sem):
+        ts = []
+        for d, engines in call:
+            c = T.cores[d]
+            rid, pid, _ = topo.addr(c)
+            a, b = src[:, w * d:w * d + w], dst[:, to:to + w]
+            if codes:
+                a, b = a.bitcast(dt.uint8), b.bitcast(dt.uint8)
+            left[0] += len(engines)
+            ts.append(RemoteDMATransfer(dst_ids=[DstId(rid=rid, pnc=pid)], dma_engine_mask=sum(1 << e for e in engines),
+                                        remote_sem=S[sem], src=a, dst=b))
+        g.remote_dma_fused(ts, local_sem=S.left)
+
+    plan = _plan(T, topo, me, "A")
+    wait(g, "pka")
+    for call in plan:
+        send(call, T.sndw, T.win, CW, own, True, "arwc")
+    wait(g, "pkas")
+    for call in plan:
+        send(call, T.sndws, T.wins, CW, own, False, "arws")
+    g.iota(T.cslot[:, :], [[16, 48]], 0, 1, allow_small_or_imprecise_dtypes=True).then_inc(S.i_s, 1)
+
+    wait(V, ("dwp", 128), "i_k", a2)
+    b1 = step(V.tensor_scalar(T.w1[:, :], T.lwp[:, :], 1023, None, Op.bitwise_and))
+    wait(V, ("drd", 128))
+    c1 = step(V.tensor_scalar(T.r1[:, 0:3], T.lrd[:, 0:3], 0.0, 16.0, Op.max, Op.mult))
+    wait(V, b1)
+    b2 = step(V.tensor_tensor(T.w2[:, :], T.w1[:, :], T.ck[:, :], Op.min))
+    wait(V, c1)
+    c2 = step(V.tensor_scalar(T.offr[:, 0:3], T.r1[:, 0:3], T.cold[:, 0:1], None, Op.add))
+    wait(V, b2)
+    b3 = step(V.tensor_scalar(T.offw[:, :], T.w2[:, :], T.cold[:, 0:1], None, Op.add))
+    wait(V, b3, "row", "i_c")
+    b4 = step(V.tensor_copy(T.srow[:, :].indirect(T.offw[:, :]), T.cnt[:, POOL:WIN]))
+    wait(V, b4)
+    b5 = step(V.transpose(T.srct[:, :], T.srow[:, 0:ROW]))
+    wait(V, "oo")
+    V.tensor_copy(T.win[:, own:own + CW].bitcast(dt.uint32), T.nwq[:, 0:NW].bitcast(dt.uint32).indirect(T.offo[:, 0:1])).then_inc(S.owna, 1)
+    wait(V, b5, c2)
+    V.tensor_copy(T.offb[:, :], T.srct[:, :].indirect(T.offr[:, 0:3])).then_inc(S.ob, 1)
+    wait(V, ("dpl", 16))
+    V.quantize_mx(T.win[:, 0:POOL], T.wins[:, 0:POOL], T.plt[:, :]).then_inc(S.plq, 1)
+
+    away, near, _, _ = _roads(T, topo, me)
+    picks = [(m[0], len(m), "sndp", "pkb%d" % k) for k, m in enumerate(away)]
+    picks += [(near[0], 1, "sndp", "pkb3"), (me, 1, "land", "ownb")]
+    wait(V, "owna", "plq", "ob", ("arwc", arrive["A"]))
+    for r, n, buf, ev in picks:
+        V.tensor_copy(T[buf][:, PC * r:PC * (r + n)].bitcast(dt.uint32),
+                      T.win[:, :].bitcast(dt.uint32).indirect(T.offb[:, CP * r:CP * (r + n)])).then_inc(S[ev], 1)
+    wait(A, "ownas", "plq", "ob", ("arws", arrive["A"]))
+    for r, n, buf, ev in picks:
+        A.activation(T[buf + "s"][:, PC * r:PC * (r + n)], T.wins[:, :].indirect(T.offb[:, CP * r:CP * (r + n)]),
+                     Copy).then_inc(S[ev.replace("pkb", "pkbs").replace("ownb", "ownbs")], 1)
+    plan = _plan(T, topo, me, "B")
+    need = ((0,), (1, 2, 3))
+    for k, call in enumerate(plan):
+        wait(g, *["pkb%d" % i for i in need[k]])
+        send(call, T.sndp, T.land, PC, PC * me, True, "arpc")
+    for k, call in enumerate(plan):
+        wait(g, *["pkbs%d" % i for i in need[k]])
+        send(call, T.sndps, T.lands, PC, PC * me, False, "arps")
+    g.wait_ge(S.left, left[0])
+
+    wait(V, ("dqw", 16))
+    V.quantize_mx(T.qwq[:, :], T.qws[:, :], T.qwt[:, :]).then_inc(S.qwd, 1)
+    wait(V, "i_p")
+    e1 = step(V.tensor_scalar(T.pand[:, 1:2], T.pcol[:, 0:1], 112, None, Op.bitwise_and))
+    wait(V, ("dpg", 128))
+    e2 = step(V.tensor_copy(T.offg[:, :], T.lpg[:, :]))
+    wait(V, e1)
+    e3 = step(V.tensor_copy(T.colg[:, :], T.pand[:, 1:2]))
+    wait(V, e3, "i_s")
+    e4 = step(V.tensor_scalar(T.wslot[:, :], T.cslot[:, :], T.colg[:, 0:1], None, Op.subtract))
+    wait(V, e2, e4)
+    V.tensor_copy(T.offc[:, :], T.wslot[:, :].indirect(T.offg[:, 0:2])).then_inc(S.oc, 1)
+
+    k = CC // 16
+    wait(V, "ownb", "oc", ("arpc", arrive["B"]))
+    for c in range(CH):
+        V.tensor_copy(T.fin[:, CC * c:CC * c + CC].bitcast(dt.uint32),
+                      T.land[:, :].bitcast(dt.uint32).indirect(T.offc[:, k * c:k * c + k])).then_inc(S["fc%d" % c], 1)
+    for q in (V, A):
+        wait(q, "ownbs", "oc", ("arps", arrive["B"]))
+    for c in range(CH):
+        a, b = T.fins[:, CC * c:CC * c + CC], T.lands[:, :].indirect(T.offc[:, k * c:k * c + k])
+        (A.activation(a, b, Copy) if c % 2 else V.tensor_copy(a, b)).then_inc(S["fs%d" % c], 1)
+    wait(P, "qwd")
+    half = [(h, o) for h in range(2) for o in range(O)]
+    for h, o in half:
+        for c in (2 * h, 2 * h + 1):
+            if o == 0:
+                wait(P, "fc%d" % c, "fs%d" % c)
+            b = O * c + o
+            P.matmul_mx(T.ps[:, 512 * b:512 * b + CC], T.qwq[:, 128 * o:128 * o + 128], T.qws[:, 128 * o:128 * o + 128],
+                        T.fin[:, CC * c:CC * c + CC], T.fins[:, CC * c:CC * c + CC], True, True).then_inc(S["mm%d" % b], 1)
+    for h, o in half:
+        for c in (2 * h, 2 * h + 1):
+            b, at = O * c + o, 512 * o + CC * c
+            q = A if c % 2 else V
+            wait(q, "mm%d" % b)
+            u, v = T.yb[:, at:at + CC], T.ps[:, 512 * b:512 * b + CC]
+            (A.activation(u, v, Copy) if c % 2 else V.tensor_copy(u, v)).then_inc(S["cp%d" % b], 1)
+            wait(Y, "cp%d" % b)
+        at = 512 * o + 2 * CC * h
+        Y.dma_start(T.y[:, at:at + 2 * CC], T.yb[:, at:at + 2 * CC]).then_inc(S.ystore, 16)
+    Y.wait_ge(S.ystore, 16 * len(half))

@@ -4,11 +4,16 @@ from concourse.mybir import dt, AluOpType, ActivationFunctionType
 N = 8
 PG, NW, SP, CW, CP, O = 32, 64, 32, 16, 6, 2
 POOL = 16 * PG
-WIN = POOL + N * CW
+SLOTS = N * CW
+NEW = SLOTS + CW
+WIN = NEW + POOL
 PC = 16 * CP
 ROW = POOL + 32
+FR = ROW // 16
 DUMP = ROW - 16
 SROW = 800
+NONE = 1024.0
+CUTS = (0, 128, 384, 512)
 CH = 4
 CC = 16 * SP // CH
 
@@ -22,32 +27,32 @@ def _sb(n, d):
 SCRATCH = {
     "nwt": _sb(512, BF), "plt": _sb(4 * POOL, BF), "qwt": _sb(512 * O, BF),
     "lwr": _sb(8, I32), "lwp": _sb(8, I32), "lrd": _sb(4, I32), "lpg": _sb(2, I32),
-    "pcol": _sb(1, I32), "pand": _sb(2, I32), "cold": _sb(1, F32), "coln": _sb(1, F32), "colg": _sb(1, F32),
-    "ck": _sb(8, I32), "cnt": _sb(WIN, F32), "cslot": _sb(48, F32), "wslot": _sb(48, F32),
-    "offa": _sb(8, U16), "offo": _sb(2, U16), "offw": _sb(8, U16), "offr": _sb(4, U16), "offb": _sb(48, U16),
-    "offg": _sb(2, U16), "offc": _sb(32, U16),
-    "w1": _sb(8, I32), "w2": _sb(8, F32), "r1": _sb(4, F32),
-    "srow": _sb(SROW, F32), "srct": _sb(ROW, F32),
+    "pcol": _sb(1, I32), "pand": _sb(2, I32), "cold": _sb(1, F32), "colq": _sb(1, F32), "colg": _sb(1, F32),
+    "colb": _sb(1, F32), "kval": _sb(SLOTS, BF), "cslot": _sb(48, F32), "wslot": _sb(48, F32), "cbase": _sb(FR, F32),
+    "offa": _sb(8, U16), "offw": _sb(8, U16), "offr": _sb(4, U16),
+    "offb": _sb(48, U16), "offg": _sb(2, U16), "offc": _sb(32, U16),
+    "w1": _sb(8, I32), "w2": _sb(8, F32), "srcf": _sb(FR, F32),
+    "srow": _sb(SROW, BF), "srct": _sb(ROW, BF),
     "nwq": _sb(128, F8), "nws": _sb(128, U8),
-    "sndw": _sb(N * CW, F8), "sndws": _sb(N * CW, U8),
+    "sndw": _sb(SLOTS, F8), "sndws": _sb(SLOTS, U8),
     "win": _sb(WIN, F8), "wins": _sb(WIN, U8),
     "sndp": _sb(N * PC, F8), "sndps": _sb(N * PC, U8),
     "land": _sb(N * PC, F8), "lands": _sb(N * PC, U8),
+    "hws": _sb(2 * CW, U8), "hp": _sb(2 * PC, F8),
     "fin": _sb(16 * SP, F8), "fins": _sb(16 * SP, U8),
     "qwq": _sb(128 * O, F8), "qws": _sb(128 * O, U8),
     "ps": ("psum", [128, 512 * CH * O], F32),
     "yb": _sb(512 * O, F32),
 }
-SEMAPHORES = (["dnw", "dwr", "dwp", "drd", "dpg", "dpl", "dqw", "ystore"]
-              + ["i_p", "i_k", "i_c", "i_s", "cn", "row"]
+SEMAPHORES = (["dnw", "dwr", "dwp", "drd", "dpg", "dpl0", "dpl1", "dpl2", "plq2", "dqw", "ystore"]
+              + ["i_p", "i_k", "i_s", "cg", "cb", "ws", "bs", "go"]
               + ["v%d" % k for k in range(24)]
-              + ["nq", "oa", "oo", "oc", "ob", "plq", "qwd",
-                 "pka", "pkas", "owna", "ownas",
-                 "ownb", "ownbs"]
-              + ["pkb%d" % k for k in range(4)] + ["pkbs%d" % k for k in range(4)]
+              + ["nq", "oa", "oc", "ob", "plq0", "plq1", "qwd", "ownb", "ownbs"]
+              + ["pka%d" % k for k in range(3)] + ["pkas%d" % k for k in range(3)]
+              + ["pkb%d" % k for k in range(6)] + ["pkbs%d" % k for k in range(6)]
               + ["fc%d" % k for k in range(CH)] + ["fs%d" % k for k in range(CH)]
               + ["mm%d" % k for k in range(CH * O)] + ["cp%d" % k for k in range(CH * O)]
-              + ["arwc", "arws", "arpc", "arps", "left"])
+              + ["arwc", "arws", "arpc", "arps", "left", "hopa", "hopb"])
 
 
 def _chips(T, topo):
@@ -72,20 +77,69 @@ def _deal(dests, engines):
     return [(d, engines[k * i:k * i + k]) for i, d in enumerate(dests)]
 
 
-def _plan(T, topo, r, phase):
+def _split(away):
+    for a in away:
+        for b in away:
+            if b[0] == a[-1] + 1:
+                return a + b, [c for c in away if c != a and c != b][0]
+
+
+def _plan(T, topo, r):
     away, near, out, inn = _roads(T, topo, r)
-    if phase == "A":
-        return [_deal(away[0] + away[1], out) + _deal(near, inn[:2]), _deal(away[2], out)]
-    return [_deal(away[0], out), _deal(away[1] + away[2], out) + _deal(near, inn[:2])]
+    four, two = _split(away)
+    return {"arwc": [_deal(two, out), _deal(four, out), _deal(near, inn)],
+            "arws": [_deal(four, out) + _deal(near, inn[4:])] + [_deal([d], out) for d in two],
+            "arpc": [_deal([d], out) for d in away[0]] + [_deal(away[2], out) + _deal(near, inn)] + [_deal([d], out) for d in away[1]],
+            "arps": [_deal(away[0] + away[1], out), _deal(away[2], out) + _deal(near, inn)]}
+
+
+H = 2
+
+
+def _helpers(T, topo, r):
+    c = T.cores[r]
+    return [k for k in topo.cores_of(c) if topo.die(k) == topo.die(c) and T.rank_of(k) is None][:H]
+
+
+def _fused(g, T, topo, ts, local):
+    out = []
+    for c, engines, a, b, sem in ts:
+        rid, pid, _ = topo.addr(c)
+        out.append(RemoteDMATransfer(dst_ids=[DstId(rid=rid, pnc=pid)], dma_engine_mask=sum(1 << e for e in engines),
+                                     remote_sem=sem, src=a, dst=b))
+    g.remote_dma_fused(out, local_sem=local)
+    return sum(len(t[1]) for t in ts)
+
+
+def _slot(T, topo, s, q):
+    first = [m[0] for m in _chips(T, topo) if q in m][0]
+    return CW * (s + (s > first))
+
+
+HOPA, HOPB = 4, 4
+
+
+def helper_program(g, r, k, T, topo):
+    S, plan = T.sem, _plan(T, topo, r)
+    g.wait_ge(S.hopa, HOPA)
+    n = _fused(g, T, topo, [(T.cores[d], e, T.hws[:, CW * i:CW * i + CW], T.wins[:, _slot(T, topo, r, d):_slot(T, topo, r, d) + CW], S.arws)
+                            for i, (d, e) in enumerate(plan["arws"][k - H])], S.left)
+    g.wait_ge(S.hopb, HOPB)
+    n += _fused(g, T, topo, [(T.cores[d], e, T.hp[:, PC * i:PC * i + PC].bitcast(dt.uint8), T.land[:, PC * r:PC * r + PC].bitcast(dt.uint8), S.arpc)
+                             for i, (d, e) in enumerate(plan["arpc"][k - H])], S.left)
+    g.wait_ge(S.left, n)
 
 
 def rank_program(g, core, T, topo):
     me = T.rank_of(core)
     if me is None:
+        for r in range(N):
+            if core in _helpers(T, topo, r):
+                helper_program(g, r, _helpers(T, topo, r).index(core), T, topo)
         return
     S = T.sem
     V, A, P, Y = g.vector, g.scalar, g.tensor, g.sync
-    Op, Copy = AluOpType, ActivationFunctionType.Copy
+    Op, Copy, Ident = AluOpType, ActivationFunctionType.Copy, ActivationFunctionType.Identity
     nv = [0]
 
     def wait(q, *evs):
@@ -99,156 +153,196 @@ def rank_program(g, core, T, topo):
         call.then_inc(S[n], 1)
         return n
 
-    arrive = {}
-    for ph in "AB":
-        arrive[ph] = sum(len(e) for r in range(N) if r != me for call in _plan(T, topo, r, ph) for d, e in call if d == me)
+    plan = _plan(T, topo, me)
+    arrive = {k: (k, sum(len(e) for r in range(N) if r != me for call in _plan(T, topo, r)[k] for d, e in call if d == me))
+              for k in plan}
+    away, near, _, _ = _roads(T, topo, me)
+    four, two = _split(away)
+    first = {r: m[0] for m in _chips(T, topo) for r in m}
+    pair = [first[me], first[me] + 1]
+    spare = CW * pair[1]
+
+    def slot(s, q):
+        return CW * (s + (s > first[q]))
 
     def table(q, dst, src, cols, sem, groups):
         for k in groups:
             q.dma_start(dst[16 * k:16 * k + 16, 0:cols], src[:, :]).then_inc(S[sem], 16)
 
+    def load_pool(k):
+        a, b = 4 * CUTS[k], 4 * CUTS[k + 1]
+        Y.dma_start(T.plt[:, a:b], T.pl[:, a:b]).then_inc(S["dpl%d" % k], 16)
+
     table(A, T.lwr, T.wr, 8, "dwr", range(0, 4))
-    A.dma_start(T.qwt[:, :], T.qw[:, :]).then_inc(S.dqw, 16)
+    table(A, T.lwp, T.wp, 8, "dwp", range(0, 5))
+    table(A, T.lrd, T.rd, 3, "drd", range(0, 1))
     Y.dma_start(T.nwt[:, 0:4 * NW], T.nw[:, :]).then_inc(S.dnw, 16)
     table(Y, T.lwr, T.wr, 8, "dwr", range(4, 8))
-    Y.dma_start(T.plt[:, :], T.pl[:, :]).then_inc(S.dpl, 16)
-    table(Y, T.lwp, T.wp, 8, "dwp", range(8))
-    table(Y, T.lrd, T.rd, 3, "drd", range(8))
+    load_pool(0)
+    table(Y, T.lwp, T.wp, 8, "dwp", range(5, 8))
+    load_pool(1)
+    table(Y, T.lrd, T.rd, 3, "drd", range(1, 8))
+    load_pool(2)
+    Y.dma_start(T.qwt[:, :], T.qw[:, :]).then_inc(S.dqw, 16)
     table(Y, T.lpg, T.pg, 2, "dpg", range(8))
 
     g.iota(T.pcol[:, :], [[1, 1]], 0, 1).then_inc(S.i_p, 1)
-    g.iota(T.ck[:, :], [[16, 8]], DUMP, 1).then_inc(S.i_k, 1)
-    g.iota(T.cnt[:, :], [[1, WIN]], 0, 0, allow_small_or_imprecise_dtypes=True).then_inc(S.i_c, 1)
-
+    g.iota(T.cslot[:, :], [[16, 48]], DUMP, 1, allow_small_or_imprecise_dtypes=True).then_inc(S.i_s, 1)
+    g.iota(T.kval[:, 0:spare], [[1, spare]], 0, 0, allow_small_or_imprecise_dtypes=True).then_inc(S.i_k, 1)
+    g.iota(T.kval[:, spare:SLOTS], [[1, SLOTS - spare]], spare + CW, 0, allow_small_or_imprecise_dtypes=True).then_inc(S.i_k, 1)
     z = step(V.memset(T.nwt[:, 4 * NW:512], 0.0))
+    row = step(V.memset(T.srow[:, 0:ROW], NONE))
     wait(V, "i_p")
     a1 = step(V.tensor_scalar(T.pand[:, 0:1], T.pcol[:, 0:1], 16, None, Op.bitwise_and))
+    a2 = step(V.tensor_scalar(T.pand[:, 1:2], T.pcol[:, 0:1], 112, None, Op.bitwise_and))
     wait(V, a1)
-    V.tensor_scalar(T.coln[:, :], T.pand[:, 0:1], 32.0, None, Op.subtract).then_inc(S.cn, 1)
-    a2 = step(V.tensor_scalar(T.cold[:, :], T.pand[:, 0:1], -1.0, 32.0, Op.mult, Op.add))
+    a3 = step(V.tensor_scalar(T.cold[:, :], T.pand[:, 0:1], -1.0, 32.0, Op.mult, Op.add))
+    a4 = step(V.tensor_scalar(T.colq[:, :], T.pand[:, 0:1], -1.0 / 16, 2.0, Op.mult, Op.add))
 
+    def pick_a(k, q):
+        m = [four, two, pair][k]
+        dst, at = (("win", slot(pair[0], me) if me == pair[0] else spare) if k == 2 else ("sndw", CW * m[0]))
+        off = T.offa[:, m[0]:m[-1] + 1]
+        if q is V:
+            V.tensor_copy(T[dst][:, at:at + CW * len(m)].bitcast(dt.uint32),
+                          T.nwq[:, 0:NW].bitcast(dt.uint32).indirect(off)).then_inc(S["pka%d" % k], 1)
+        else:
+            A.activation(T[dst + "s"][:, at:at + CW * len(m)], T.nws[:, 0:NW].indirect(off), Copy).then_inc(S["pkas%d" % k], 1)
+
+    wait(V, a2)
+    V.tensor_scalar(T.colg[:, :], T.pand[:, 1:2], -1.0, -float(DUMP), Op.mult, Op.add).then_inc(S.cg, 1)
+    wait(V, "cg", a3)
+    V.tensor_scalar(T.colb[:, :], T.colg[:, :], T.cold[:, 0:1], float(NEW), Op.subtract, Op.add).then_inc(S.cb, 1)
     wait(V, ("dwr", 128))
     V.tensor_copy(T.offa[:, :], T.lwr[:, :]).then_inc(S.oa, 1)
     wait(V, z, ("dnw", 16))
     V.quantize_mx(T.nwq[:, :], T.nws[:, :], T.nwt[:, :]).then_inc(S.nq, 1)
-    wait(V, "oa", "nq")
-    V.tensor_copy(T.sndw[:, :].bitcast(dt.uint32), T.nwq[:, 0:NW].bitcast(dt.uint32).indirect(T.offa[:, 0:8])).then_inc(S.pka, 1)
-    V.tensor_copy(T.offo[:, 0:1], T.lwr[:, me:me + 1]).then_inc(S.oo, 1)
-    own = POOL + CW * me
-
-    wait(A, "oa", "nq")
-    A.activation(T.sndws[:, :], T.nws[:, 0:NW].indirect(T.offa[:, 0:8]), Copy).then_inc(S.pkas, 1)
-    wait(A, "i_c", "cn")
-    A.activation(T.srow[:, 0:ROW], T.cnt[:, 0:ROW], ActivationFunctionType.Identity, bias=T.coln[:, 0:1]).then_inc(S.row, 1)
-    wait(A, "oo")
-    A.activation(T.wins[:, own:own + CW], T.nws[:, 0:NW].indirect(T.offo[:, 0:1]), Copy).then_inc(S.ownas, 1)
+    wait(V, "nq", "oa")
+    for k in (1, 0, 2):
+        pick_a(k, V)
+    wait(V, ("dwp", 128), "i_s", a3)
+    b1 = step(V.tensor_scalar(T.w1[:, :], T.lwp[:, :], 1023, None, Op.bitwise_and))
+    wait(A, "nq", "oa")
+    for k in (1, 0, 2):
+        pick_a(k, A)
 
     left = [0]
+    inn = _roads(T, topo, me)[3]
 
-    def send(call, src, dst, w, to, codes, sem):
-        ts = []
-        for d, engines in call:
-            c = T.cores[d]
-            rid, pid, _ = topo.addr(c)
-            a, b = src[:, w * d:w * d + w], dst[:, to:to + w]
-            if codes:
-                a, b = a.bitcast(dt.uint8), b.bitcast(dt.uint8)
-            left[0] += len(engines)
-            ts.append(RemoteDMATransfer(dst_ids=[DstId(rid=rid, pnc=pid)], dma_engine_mask=sum(1 << e for e in engines),
-                                        remote_sem=S[sem], src=a, dst=b))
-        g.remote_dma_fused(ts, local_sem=S.left)
+    def send(call, src, dst, codes, sem, more=()):
+        ts = [(T.cores[d], e, src(d), dst(d), S[sem]) for d, e in call] + list(more)
+        if codes:
+            ts = [(c, e, a.bitcast(dt.uint8), b.bitcast(dt.uint8), s) for c, e, a, b, s in ts]
+        left[0] += _fused(g, T, topo, ts, S.left)
 
-    plan = _plan(T, topo, me, "A")
-    wait(g, "pka")
-    for call in plan:
-        send(call, T.sndw, T.win, CW, own, True, "arwc")
-    wait(g, "pkas")
-    for call in plan:
-        send(call, T.sndws, T.wins, CW, own, False, "arws")
-    g.iota(T.cslot[:, :], [[16, 48]], 0, 1, allow_small_or_imprecise_dtypes=True).then_inc(S.i_s, 1)
+    def send_a(call, codes, more=()):
+        snd, win = (T.sndw, T.win) if codes else (T.sndws, T.wins)
+        send(call, lambda d: win[:, spare:spare + CW] if d in near else snd[:, CW * d:CW * d + CW],
+             lambda d: win[:, slot(me, d):slot(me, d) + CW], codes, "arwc" if codes else "arws", more)
 
-    wait(V, ("dwp", 128), "i_k", a2)
-    b1 = step(V.tensor_scalar(T.w1[:, :], T.lwp[:, :], 1023, None, Op.bitwise_and))
-    wait(V, ("drd", 128))
-    c1 = step(V.tensor_scalar(T.r1[:, 0:3], T.lrd[:, 0:3], 0.0, 16.0, Op.max, Op.mult))
+    wait(g, "pka1")
+    send_a(plan["arwc"][0], True)
+    wait(g, "pka0")
+    send_a(plan["arwc"][1], True)
+    wait(g, "pkas1")
+    send_a([], False, [(c, e, T.sndws[:, CW * d:CW * d + CW], T.hws[:, 0:CW], S.hopa)
+                       for (c, e), d in zip(_deal(_helpers(T, topo, me), inn[:H * HOPA]), two)])
+    wait(g, "pka2")
+    send_a(plan["arwc"][2], True)
+    wait(g, "pkas0", "pkas2")
+    send_a(plan["arws"][0], False)
+
+    def pool(k):
+        a, b = CUTS[k], CUTS[k + 1]
+        wait(V, ("dpl%d" % k, 16))
+        V.quantize_mx(T.win[:, NEW + a:NEW + b], T.wins[:, NEW + a:NEW + b], T.plt[:, 4 * a:4 * b]).then_inc(S["plq%d" % k], 1)
+
+    pool(0)
     wait(V, b1)
-    b2 = step(V.tensor_tensor(T.w2[:, :], T.w1[:, :], T.ck[:, :], Op.min))
-    wait(V, c1)
-    c2 = step(V.tensor_scalar(T.offr[:, 0:3], T.r1[:, 0:3], T.cold[:, 0:1], None, Op.add))
+    b2 = step(V.tensor_tensor(T.w2[:, :], T.w1[:, :], T.cslot[:, 0:8], Op.min))
     wait(V, b2)
     b3 = step(V.tensor_scalar(T.offw[:, :], T.w2[:, :], T.cold[:, 0:1], None, Op.add))
-    wait(V, b3, "row", "i_c")
-    b4 = step(V.tensor_copy(T.srow[:, :].indirect(T.offw[:, :]), T.cnt[:, POOL:WIN]))
+    wait(V, b3, row, ("i_k", 2))
+    b4 = step(V.tensor_copy(T.srow[:, :].indirect(T.offw[:, :]), T.kval[:, :]))
+    pool(1)
     wait(V, b4)
     b5 = step(V.transpose(T.srct[:, :], T.srow[:, 0:ROW]))
-    wait(V, "oo")
-    V.tensor_copy(T.win[:, own:own + CW].bitcast(dt.uint32), T.nwq[:, 0:NW].bitcast(dt.uint32).indirect(T.offo[:, 0:1])).then_inc(S.owna, 1)
-    wait(V, b5, c2)
-    V.tensor_copy(T.offb[:, :], T.srct[:, :].indirect(T.offr[:, 0:3])).then_inc(S.ob, 1)
-    wait(V, ("dpl", 16))
-    V.quantize_mx(T.win[:, 0:POOL], T.wins[:, 0:POOL], T.plt[:, :]).then_inc(S.plq, 1)
+    wait(V, ("drd", 128), a4)
+    c1 = step(V.tensor_scalar(T.offr[:, 0:3], T.lrd[:, 0:3], T.colq[:, 0:1], None, Op.add))
+    wait(V, b5, "bs")
+    b6 = step(V.tensor_tensor(T.srcf[:, :], T.srct[:, 0:ROW:16], T.cbase[:, :], Op.min))
+    pool(2)
+    wait(V, b6, c1)
+    V.tensor_copy(T.offb[:, :], T.srcf[:, :].indirect(T.offr[:, 0:3])).then_inc(S.ob, 1)
 
-    away, near, _, _ = _roads(T, topo, me)
-    picks = [(m[0], len(m), "sndp", "pkb%d" % k) for k, m in enumerate(away)]
-    picks += [(near[0], 1, "sndp", "pkb3"), (me, 1, "land", "ownb")]
-    wait(V, "owna", "plq", "ob", ("arwc", arrive["A"]))
-    for r, n, buf, ev in picks:
-        V.tensor_copy(T[buf][:, PC * r:PC * (r + n)].bitcast(dt.uint32),
-                      T.win[:, :].bitcast(dt.uint32).indirect(T.offb[:, CP * r:CP * (r + n)])).then_inc(S[ev], 1)
-    wait(A, "ownas", "plq", "ob", ("arws", arrive["A"]))
-    for r, n, buf, ev in picks:
-        A.activation(T[buf + "s"][:, PC * r:PC * (r + n)], T.wins[:, :].indirect(T.offb[:, CP * r:CP * (r + n)]),
-                     Copy).then_inc(S[ev.replace("pkb", "pkbs").replace("ownb", "ownbs")], 1)
-    plan = _plan(T, topo, me, "B")
-    need = ((0,), (1, 2, 3))
-    for k, call in enumerate(plan):
-        wait(g, *["pkb%d" % i for i in need[k]])
-        send(call, T.sndp, T.land, PC, PC * me, True, "arpc")
-    for k, call in enumerate(plan):
-        wait(g, *["pkbs%d" % i for i in need[k]])
-        send(call, T.sndps, T.lands, PC, PC * me, False, "arps")
+    wait(A, "i_s", "cb")
+    A.activation(T.cbase[:, :], T.cslot[:, 0:FR], Ident, bias=T.colb[:, 0:1]).then_inc(S.bs, 1)
+    wait(A, "cg")
+    A.activation(T.wslot[:, :], T.cslot[:, :], Ident, bias=T.colg[:, 0:1]).then_inc(S.ws, 1)
+
+    picks = [([d], "sndp") for d in away[0]] + [(away[1], "sndp"), (away[2], "sndp"), (near, "sndp"), ([me], "land")]
+
+    def pick_b(k, q, codes):
+        m, buf = picks[k]
+        a, b, off = PC * m[0], PC * (m[-1] + 1), T.offb[:, CP * m[0]:CP * (m[-1] + 1)]
+        if codes:
+            V.tensor_copy(T[buf][:, a:b].bitcast(dt.uint32), T.win[:, :].bitcast(dt.uint32).indirect(off)).then_inc(S["pkb%d" % k], 1)
+        elif q is V:
+            V.tensor_copy(T[buf + "s"][:, a:b], T.wins[:, :].indirect(off)).then_inc(S["pkbs%d" % k], 1)
+        else:
+            A.activation(T[buf + "s"][:, a:b], T.wins[:, :].indirect(off), Copy).then_inc(S["pkbs%d" % k], 1)
+
+    wait(V, "pka2", "plq0", "plq1", "plq2", "ob", arrive["arwc"])
+    for k in range(len(picks)):
+        pick_b(k, V, True)
+    for q, part in ((A, (0, 1, 3, 5)), (V, (2, 4))):
+        wait(q, "pkas2", "plq0", "plq1", "plq2", "ob", arrive["arws"])
+        for k in part:
+            pick_b(k, q, False)
+    hop = [(c, e, T.sndp[:, PC * d:PC * d + PC], T.hp[:, 0:PC], S.hopb)
+           for (c, e), d in zip(_deal(_helpers(T, topo, me), inn[:H * HOPB]), away[1])]
+    codes, scales = plan["arpc"], plan["arps"]
+    for need, call, more in (((0,), codes[0], ()), ((1,), codes[1], ()), ((2,), [], hop), ((3, 4), codes[2], ())):
+        wait(g, *["pkb%d" % k for k in need])
+        send(call, lambda d: T.sndp[:, PC * d:PC * d + PC], lambda d: T.land[:, PC * me:PC * me + PC], True, "arpc", more)
+    for need, call in (((0, 1, 2), scales[0]), ((3, 4), scales[1])):
+        wait(g, *["pkbs%d" % k for k in need])
+        send(call, lambda d: T.sndps[:, PC * d:PC * d + PC], lambda d: T.lands[:, PC * me:PC * me + PC], False, "arps")
     g.wait_ge(S.left, left[0])
 
-    wait(V, ("dqw", 16))
-    V.quantize_mx(T.qwq[:, :], T.qws[:, :], T.qwt[:, :]).then_inc(S.qwd, 1)
-    wait(V, "i_p")
-    e1 = step(V.tensor_scalar(T.pand[:, 1:2], T.pcol[:, 0:1], 112, None, Op.bitwise_and))
     wait(V, ("dpg", 128))
     e2 = step(V.tensor_copy(T.offg[:, :], T.lpg[:, :]))
-    wait(V, e1)
-    e3 = step(V.tensor_copy(T.colg[:, :], T.pand[:, 1:2]))
-    wait(V, e3, "i_s")
-    e4 = step(V.tensor_scalar(T.wslot[:, :], T.cslot[:, :], T.colg[:, 0:1], None, Op.subtract))
-    wait(V, e2, e4)
+    wait(V, e2, "ws")
     V.tensor_copy(T.offc[:, :], T.wslot[:, :].indirect(T.offg[:, 0:2])).then_inc(S.oc, 1)
+    wait(V, ("dqw", 16))
+    V.quantize_mx(T.qwq[:, :], T.qws[:, :], T.qwt[:, :]).then_inc(S.qwd, 1)
 
     k = CC // 16
-    wait(V, "ownb", "oc", ("arpc", arrive["B"]))
+    wait(V, "pkb5", "oc", arrive["arpc"])
     for c in range(CH):
         V.tensor_copy(T.fin[:, CC * c:CC * c + CC].bitcast(dt.uint32),
                       T.land[:, :].bitcast(dt.uint32).indirect(T.offc[:, k * c:k * c + k])).then_inc(S["fc%d" % c], 1)
-    for q in (V, A):
-        wait(q, "ownbs", "oc", ("arps", arrive["B"]))
+    wait(A, "pkbs5", "oc", arrive["arps"])
     for c in range(CH):
-        a, b = T.fins[:, CC * c:CC * c + CC], T.lands[:, :].indirect(T.offc[:, k * c:k * c + k])
-        (A.activation(a, b, Copy) if c % 2 else V.tensor_copy(a, b)).then_inc(S["fs%d" % c], 1)
+        A.activation(T.fins[:, CC * c:CC * c + CC], T.lands[:, :].indirect(T.offc[:, k * c:k * c + k]), Copy).then_inc(S["fs%d" % c], 1)
     wait(P, "qwd")
-    half = [(h, o) for h in range(2) for o in range(O)]
-    for h, o in half:
-        for c in (2 * h, 2 * h + 1):
-            if o == 0:
-                wait(P, "fc%d" % c, "fs%d" % c)
-            b = O * c + o
-            P.matmul_mx(T.ps[:, 512 * b:512 * b + CC], T.qwq[:, 128 * o:128 * o + 128], T.qws[:, 128 * o:128 * o + 128],
-                        T.fin[:, CC * c:CC * c + CC], T.fins[:, CC * c:CC * c + CC], True, True).then_inc(S["mm%d" % b], 1)
-    for h, o in half:
-        for c in (2 * h, 2 * h + 1):
+    stores = [(1, (0,)), (0, (0, 1)), (1, (1, 2)), (0, (2, 3)), (1, (3,))]
+    ready = []
+    for o, c in [(o, c) for o, cs in stores for c in cs]:
+        if c not in ready:
+            ready.append(c)
+            wait(P, "fc%d" % c, "fs%d" % c)
+        b = O * c + o
+        P.matmul_mx(T.ps[:, 512 * b:512 * b + CC], T.qwq[:, 128 * o:128 * o + 128], T.qws[:, 128 * o:128 * o + 128],
+                    T.fin[:, CC * c:CC * c + CC], T.fins[:, CC * c:CC * c + CC], True, True).then_inc(S["mm%d" % b], 1)
+    for o, cs in stores:
+        for c in cs:
             b, at = O * c + o, 512 * o + CC * c
-            q = A if c % 2 else V
+            q = A if (o, c) == (1, 3) else V
             wait(q, "mm%d" % b)
-            u, v = T.yb[:, at:at + CC], T.ps[:, 512 * b:512 * b + CC]
-            (A.activation(u, v, Copy) if c % 2 else V.tensor_copy(u, v)).then_inc(S["cp%d" % b], 1)
+            a, v = T.yb[:, at:at + CC], T.ps[:, 512 * b:512 * b + CC]
+            (A.activation(a, v, Copy) if q is A else V.tensor_copy(a, v)).then_inc(S["cp%d" % b], 1)
             wait(Y, "cp%d" % b)
-        at = 512 * o + 2 * CC * h
-        Y.dma_start(T.y[:, at:at + 2 * CC], T.yb[:, at:at + 2 * CC]).then_inc(S.ystore, 16)
-    Y.wait_ge(S.ystore, 16 * len(half))
+        a, b = 512 * o + CC * cs[0], 512 * o + CC * (cs[-1] + 1)
+        Y.dma_start(T.y[:, a:b], T.yb[:, a:b]).then_inc(S.ystore, 16)
+    Y.wait_ge(S.ystore, 16 * len(stores))

@@ -13,9 +13,11 @@ FR = ROW // 16
 DUMP = ROW - 16
 SROW = 800
 NONE = 1024.0
-CUTS = (0, 128, 384, 512)
 CH = 4
-CC = 16 * SP // CH
+CC = POOL // CH
+H = 2
+JOBS = 3
+LENT = 32
 
 F8, U8, U16, I32, F32, BF = "float8_e4m3fn_x4", "uint8", "uint16", "int32", "float32", "bfloat16"
 
@@ -26,33 +28,32 @@ def _sb(n, d):
 
 SCRATCH = {
     "nwt": _sb(512, BF), "plt": _sb(4 * POOL, BF), "qwt": _sb(512 * O, BF),
-    "lwr": _sb(8, I32), "lwp": _sb(8, I32), "lrd": _sb(4, I32), "lpg": _sb(2, I32),
-    "pcol": _sb(1, I32), "pand": _sb(2, I32), "cold": _sb(1, F32), "colq": _sb(1, F32), "colg": _sb(1, F32),
+    "lwr": _sb(8, I32), "lwp": _sb(11, I32), "lpg": _sb(2, I32),
+    "pcol": _sb(1, I32), "pand": _sb(3, I32), "cold": _sb(1, F32), "colq": _sb(1, F32), "colg": _sb(1, F32),
     "colb": _sb(1, F32), "kval": _sb(SLOTS, BF), "cslot": _sb(48, F32), "wslot": _sb(48, F32), "cbase": _sb(FR, F32),
     "offa": _sb(8, U16), "offw": _sb(8, U16), "offr": _sb(4, U16),
     "offb": _sb(48, U16), "offg": _sb(2, U16), "offc": _sb(32, U16),
-    "w1": _sb(8, I32), "w2": _sb(8, F32), "srcf": _sb(FR, F32),
+    "w1": _sb(11, I32), "w2": _sb(8, F32), "srcf": _sb(FR, F32),
     "srow": _sb(SROW, BF), "srct": _sb(ROW, BF),
-    "nwq": _sb(128, F8), "nws": _sb(128, U8),
+    "nwq": _sb(128, F8), "nwqs": _sb(128, U8),
     "sndw": _sb(SLOTS, F8), "sndws": _sb(SLOTS, U8),
     "win": _sb(WIN, F8), "wins": _sb(WIN, U8),
     "sndp": _sb(N * PC, F8), "sndps": _sb(N * PC, U8),
     "land": _sb(N * PC, F8), "lands": _sb(N * PC, U8),
-    "hws": _sb(2 * CW, U8), "hp": _sb(2 * PC, F8),
+    "hws": _sb(2 * CW, U8), "hp": _sb(JOBS * 2 * PC, F8),
     "fin": _sb(16 * SP, F8), "fins": _sb(16 * SP, U8),
     "qwq": _sb(128 * O, F8), "qws": _sb(128 * O, U8),
     "ps": ("psum", [128, 512 * CH * O], F32),
     "yb": _sb(512 * O, F32),
 }
-SEMAPHORES = (["dnw", "dwr", "dwp", "drd", "dpg", "dpl0", "dpl1", "dpl2", "plq2", "dqw", "ystore"]
-              + ["i_p", "i_k", "i_s", "cg", "cb", "ws", "bs", "go"]
-              + ["v%d" % k for k in range(24)]
-              + ["nq", "oa", "oc", "ob", "plq0", "plq1", "qwd", "ownb", "ownbs"]
-              + ["pka%d" % k for k in range(3)] + ["pkas%d" % k for k in range(3)]
-              + ["pkb%d" % k for k in range(6)] + ["pkbs%d" % k for k in range(6)]
+KINDS = ("wc", "ws", "pc", "ps")
+WIDE = {"w": CW, "p": PC}
+SEMAPHORES = (["dnw", "dwr", "dwp", "dpg", "dqw", "ystore"] + ["dpl%d" % k for k in range(CH)] + ["plq%d" % k for k in range(CH)]
+              + ["i_p", "i_k", "i_s", "cg", "cb", "cw", "bs", "rep", "og", "nq", "oa", "oc", "ob", "qwd"]
+              + ["v%d" % k for k in range(16)] + ["pk%d" % k for k in range(3 * N)]
               + ["fc%d" % k for k in range(CH)] + ["fs%d" % k for k in range(CH)]
               + ["mm%d" % k for k in range(CH * O)] + ["cp%d" % k for k in range(CH * O)]
-              + ["arwc", "arws", "arpc", "arps", "left", "hopa", "hopb"])
+              + ["ar" + k for k in KINDS] + ["left"] + ["hop%d" % k for k in range(JOBS)])
 
 
 def _chips(T, topo):
@@ -66,34 +67,46 @@ def _roads(T, topo, r):
     chips = _chips(T, topo)
     at = [k for k, m in enumerate(chips) if r in m][0]
     away = [chips[(at + k) % len(chips)] for k in range(1, len(chips))]
-    near = [q for q in chips[at] if q != r]
+    near = [q for q in chips[at] if q != r][0]
     out = topo.engines(T.cores[r], T.cores[away[0][0]])
-    inn = [e for e in topo.engines(T.cores[r], T.cores[near[0]]) if e not in out]
+    inn = [e for e in topo.engines(T.cores[r], T.cores[near]) if e not in out]
     return away, near, out, inn
 
 
-def _deal(dests, engines):
-    k = len(engines) // len(dests)
-    return [(d, engines[k * i:k * i + k]) for i, d in enumerate(dests)]
+def _run(kind, m):
+    return WIDE[kind[0]] * m[0], WIDE[kind[0]] * (m[-1] + 1)
 
 
-def _split(away):
-    for a in away:
-        for b in away:
-            if b[0] == a[-1] + 1:
-                return a + b, [c for c in away if c != a and c != b][0]
+def _parts(kind, run):
+    w = WIDE[kind[0]]
+    parts = [(max(run[0], w * d), min(run[1], w * d + w)) for d in range(run[0] // w, (run[1] - 1) // w + 1)]
+    return sorted(parts, key=lambda p: p[0] - p[1])
+
+
+def _deal(kind, runs, engines, via=None):
+    k = len(engines) // len(runs)
+    return [(kind, run, via, engines[k * i:k * i + k]) for i, run in enumerate(runs)]
 
 
 def _plan(T, topo, r):
     away, near, out, inn = _roads(T, topo, r)
-    four, two = _split(away)
-    return {"arwc": [_deal(two, out), _deal(four, out), _deal(near, inn)],
-            "arws": [_deal(four, out) + _deal(near, inn[4:])] + [_deal([d], out) for d in two],
-            "arpc": [_deal([d], out) for d in away[0]] + [_deal(away[2], out) + _deal(near, inn)] + [_deal([d], out) for d in away[1]],
-            "arps": [_deal(away[0] + away[1], out), _deal(away[2], out) + _deal(near, inn)]}
+    own = [[d for d in m if topo.die(T.cores[d]) == topo.die(T.cores[r])][0] for m in away]
+    far = [[d for d in m if d not in own][0] for m in away]
 
+    def each(kind, ds, engines, via=None):
+        return _deal(kind, [_run(kind, [d]) for d in ds], engines, via)
 
-H = 2
+    a = [each("wc", far[:1], out), each("wc", away[1] + away[2], out),
+         _deal("ws", [_run("ws", away[1])], inn, 0), each("ws", far[2:], inn, 1),
+         each("wc", [near], inn) + each("wc", own[:1], out),
+         each("ws", own[2:], out) + each("ws", [near], inn)] + [each("ws", [d], out) for d in away[0]]
+    lo, hi = _run("pc", away[0])
+    kept, lent = ((lo, lo + PC - LENT), (lo + PC - LENT, hi)) if far[0] < own[0] else ((hi - PC + LENT, hi), (lo, hi - PC + LENT))
+    scales = [each("ps", m, out) for m in away]
+    b = [_deal("pc", [kept], out), _deal("pc", [lent], inn, 0), each("pc", far[1:2], out), each("pc", own[1:2], inn, 1),
+         each("pc", own[2:], inn, 0), each("pc", far[2:], out),
+         scales[1], each("pc", [near], inn), scales[2], scales[0], each("ps", [near], inn)]
+    return a, b
 
 
 def _helpers(T, topo, r):
@@ -101,14 +114,15 @@ def _helpers(T, topo, r):
     return [k for k in topo.cores_of(c) if topo.die(k) == topo.die(c) and T.rank_of(k) is None][:H]
 
 
-def _fused(g, T, topo, ts, local):
-    out = []
-    for c, engines, a, b, sem in ts:
-        rid, pid, _ = topo.addr(c)
-        out.append(RemoteDMATransfer(dst_ids=[DstId(rid=rid, pnc=pid)], dma_engine_mask=sum(1 << e for e in engines),
-                                     remote_sem=sem, src=a, dst=b))
-    g.remote_dma_fused(out, local_sem=local)
-    return sum(len(t[1]) for t in ts)
+def _jobs(T, topo, r, h):
+    return [t for call in sum(_plan(T, topo, r), []) for t in call if t[2] == h]
+
+
+def _onward(T, topo, r, job):
+    out, parts = _roads(T, topo, r)[2], _parts(*job[:2])
+    if len({b - a for a, b in parts}) == 1:
+        return [_deal(job[0], parts, out)]
+    return [_deal(job[0], [p], out) for p in parts]
 
 
 def _slot(T, topo, s, q):
@@ -116,18 +130,34 @@ def _slot(T, topo, s, q):
     return CW * (s + (s > first))
 
 
-HOPA, HOPB = 4, 4
+def _view(T, kind, names, at, run):
+    v = T[names[kind[0] == "p"] + ("s" if kind[1] == "s" else "")][:, at:at + run[1] - run[0]]
+    return v.bitcast(dt.uint8) if kind[1] == "c" else v
 
 
-def helper_program(g, r, k, T, topo):
-    S, plan = T.sem, _plan(T, topo, r)
-    g.wait_ge(S.hopa, HOPA)
-    n = _fused(g, T, topo, [(T.cores[d], e, T.hws[:, CW * i:CW * i + CW], T.wins[:, _slot(T, topo, r, d):_slot(T, topo, r, d) + CW], S.arws)
-                            for i, (d, e) in enumerate(plan["arws"][k - H])], S.left)
-    g.wait_ge(S.hopb, HOPB)
-    n += _fused(g, T, topo, [(T.cores[d], e, T.hp[:, PC * i:PC * i + PC].bitcast(dt.uint8), T.land[:, PC * r:PC * r + PC].bitcast(dt.uint8), S.arpc)
-                             for i, (d, e) in enumerate(plan["arpc"][k - H])], S.left)
-    g.wait_ge(S.left, n)
+def _landing(T, topo, s, kind, run):
+    q, at = divmod(run[0], WIDE[kind[0]])
+    return T.cores[q], _view(T, kind, ("win", "land"), at + (PC * s if kind[0] == "p" else _slot(T, topo, s, q)), run), T.sem["ar" + kind]
+
+
+def _fused(g, T, topo, ts):
+    out = []
+    for engines, a, c, b, sem in ts:
+        rid, pid, _ = topo.addr(c)
+        out.append(RemoteDMATransfer(dst_ids=[DstId(rid=rid, pnc=pid)], dma_engine_mask=sum(1 << e for e in engines),
+                                     remote_sem=sem, src=a, dst=b))
+    g.remote_dma_fused(out, local_sem=T.sem.left)
+    return sum(len(t[0]) for t in ts)
+
+
+def helper_program(g, r, h, T, topo):
+    n = 0
+    for j, job in enumerate(_jobs(T, topo, r, h)):
+        g.wait_ge(T.sem["hop%d" % j], len(job[3]))
+        for call in _onward(T, topo, r, job):
+            n += _fused(g, T, topo, [(e, _view(T, kind, ("hw", "hp"), 2 * PC * j + run[0] - job[1][0], run)) + _landing(T, topo, r, kind, run)
+                                     for kind, run, _, e in call])
+    g.wait_ge(T.sem.left, n)
 
 
 def rank_program(g, core, T, topo):
@@ -153,113 +183,109 @@ def rank_program(g, core, T, topo):
         call.then_inc(S[n], 1)
         return n
 
-    plan = _plan(T, topo, me)
-    arrive = {k: (k, sum(len(e) for r in range(N) if r != me for call in _plan(T, topo, r)[k] for d, e in call if d == me))
-              for k in plan}
-    away, near, _, _ = _roads(T, topo, me)
-    four, two = _split(away)
-    first = {r: m[0] for m in _chips(T, topo) for r in m}
-    pair = [first[me], first[me] + 1]
+    away, near, out, inn = _roads(T, topo, me)
+    plan_a, plan_b = _plan(T, topo, me)
+    arrive = {kind: 0 for kind in KINDS}
+    for r in range(N):
+        for t in [t for call in sum(_plan(T, topo, r), []) for t in call]:
+            for kind, run, _, e in [t] if t[2] is None else sum(_onward(T, topo, r, t), []):
+                arrive[kind] += len(e) * (run[0] // WIDE[kind[0]] == me)
+    arrive = {kind: ("ar" + kind, n) for kind, n in arrive.items()}
+    pair = sorted([me, near])
     spare = CW * pair[1]
+    quads = [slice(32 * k, 32 * k + 32) for k in range(4)]
 
-    def slot(s, q):
-        return CW * (s + (s > first[q]))
-
-    def table(q, dst, src, cols, sem, groups):
+    def table(q, dst, src, at, cols, sem, groups):
         for k in groups:
-            q.dma_start(dst[16 * k:16 * k + 16, 0:cols], src[:, :]).then_inc(S[sem], 16)
+            q.dma_start(dst[16 * k:16 * k + 16, at:at + cols], src[:, :]).then_inc(S[sem], 16)
 
-    def load_pool(k):
-        a, b = 4 * CUTS[k], 4 * CUTS[k + 1]
-        Y.dma_start(T.plt[:, a:b], T.pl[:, a:b]).then_inc(S["dpl%d" % k], 16)
-
-    table(A, T.lwr, T.wr, 8, "dwr", range(0, 4))
-    table(A, T.lwp, T.wp, 8, "dwp", range(0, 5))
-    table(A, T.lrd, T.rd, 3, "drd", range(0, 1))
+    table(A, T.lwr, T.wr, 0, 8, "dwr", [0, 1])
+    table(A, T.lwp, T.wp, 0, 8, "dwp", [0, 1])
+    table(A, T.lwp, T.rd, 8, 3, "dwp", [0])
     Y.dma_start(T.nwt[:, 0:4 * NW], T.nw[:, :]).then_inc(S.dnw, 16)
-    table(Y, T.lwr, T.wr, 8, "dwr", range(4, 8))
-    load_pool(0)
-    table(Y, T.lwp, T.wp, 8, "dwp", range(5, 8))
-    load_pool(1)
-    table(Y, T.lrd, T.rd, 3, "drd", range(1, 8))
-    load_pool(2)
+    table(Y, T.lwr, T.wr, 0, 8, "dwr", [2, 3])
+    for k in range(CH):
+        Y.dma_start(T.plt[:, 4 * CC * k:4 * CC * (k + 1)], T.pl[:, 4 * CC * k:4 * CC * (k + 1)]).then_inc(S["dpl%d" % k], 16)
+        if k == 0:
+            table(Y, T.lwp, T.rd, 8, 3, "dwp", [1])
     Y.dma_start(T.qwt[:, :], T.qw[:, :]).then_inc(S.dqw, 16)
-    table(Y, T.lpg, T.pg, 2, "dpg", range(8))
+    table(Y, T.lpg, T.pg, 0, 2, "dpg", [0, 1])
 
     g.iota(T.pcol[:, :], [[1, 1]], 0, 1).then_inc(S.i_p, 1)
     g.iota(T.cslot[:, :], [[16, 48]], DUMP, 1, allow_small_or_imprecise_dtypes=True).then_inc(S.i_s, 1)
     g.iota(T.kval[:, 0:spare], [[1, spare]], 0, 0, allow_small_or_imprecise_dtypes=True).then_inc(S.i_k, 1)
     g.iota(T.kval[:, spare:SLOTS], [[1, SLOTS - spare]], spare + CW, 0, allow_small_or_imprecise_dtypes=True).then_inc(S.i_k, 1)
-    z = step(V.memset(T.nwt[:, 4 * NW:512], 0.0))
     row = step(V.memset(T.srow[:, 0:ROW], NONE))
     wait(V, "i_p")
-    a1 = step(V.tensor_scalar(T.pand[:, 0:1], T.pcol[:, 0:1], 16, None, Op.bitwise_and))
-    a2 = step(V.tensor_scalar(T.pand[:, 1:2], T.pcol[:, 0:1], 112, None, Op.bitwise_and))
-    wait(V, a1)
+    bits = [step(V.tensor_scalar(T.pand[:, k:k + 1], T.pcol[:, 0:1], m, None, Op.bitwise_and)) for k, m in enumerate((16, 112, 96))]
+    z = step(V.memset(T.nwt[:, 4 * NW:512], 0.0))
+    wait(V, *bits)
     a3 = step(V.tensor_scalar(T.cold[:, :], T.pand[:, 0:1], -1.0, 32.0, Op.mult, Op.add))
     a4 = step(V.tensor_scalar(T.colq[:, :], T.pand[:, 0:1], -1.0 / 16, 2.0, Op.mult, Op.add))
-
-    def pick_a(k, q):
-        m = [four, two, pair][k]
-        dst, at = (("win", slot(pair[0], me) if me == pair[0] else spare) if k == 2 else ("sndw", CW * m[0]))
-        off = T.offa[:, m[0]:m[-1] + 1]
-        if q is V:
-            V.tensor_copy(T[dst][:, at:at + CW * len(m)].bitcast(dt.uint32),
-                          T.nwq[:, 0:NW].bitcast(dt.uint32).indirect(off)).then_inc(S["pka%d" % k], 1)
-        else:
-            A.activation(T[dst + "s"][:, at:at + CW * len(m)], T.nws[:, 0:NW].indirect(off), Copy).then_inc(S["pkas%d" % k], 1)
-
-    wait(V, a2)
     V.tensor_scalar(T.colg[:, :], T.pand[:, 1:2], -1.0, -float(DUMP), Op.mult, Op.add).then_inc(S.cg, 1)
-    wait(V, "cg", a3)
-    V.tensor_scalar(T.colb[:, :], T.colg[:, :], T.cold[:, 0:1], float(NEW), Op.subtract, Op.add).then_inc(S.cb, 1)
-    wait(V, ("dwr", 128))
-    V.tensor_copy(T.offa[:, :], T.lwr[:, :]).then_inc(S.oa, 1)
-    wait(V, z, ("dnw", 16))
-    V.quantize_mx(T.nwq[:, :], T.nws[:, :], T.nwt[:, :]).then_inc(S.nq, 1)
-    wait(V, "nq", "oa")
-    for k in (1, 0, 2):
-        pick_a(k, V)
-    wait(V, ("dwp", 128), "i_s", a3)
-    b1 = step(V.tensor_scalar(T.w1[:, :], T.lwp[:, :], 1023, None, Op.bitwise_and))
-    wait(A, "nq", "oa")
-    for k in (1, 0, 2):
-        pick_a(k, A)
+    V.tensor_scalar(T.colb[:, :], T.pand[:, 2:3], -1.0, float(NEW - DUMP - 32), Op.mult, Op.add).then_inc(S.cb, 1)
 
-    left = [0]
-    inn = _roads(T, topo, me)[3]
-
-    def send(call, src, dst, codes, sem, more=()):
-        ts = [(T.cores[d], e, src(d), dst(d), S[sem]) for d, e in call] + list(more)
+    def gather(q, codes, dst, a, b, src, n, off):
         if codes:
-            ts = [(c, e, a.bitcast(dt.uint8), b.bitcast(dt.uint8), s) for c, e, a, b, s in ts]
-        left[0] += _fused(g, T, topo, ts, S.left)
+            return V.tensor_copy(T[dst][:, a:b].bitcast(dt.uint32), T[src][:, 0:n].bitcast(dt.uint32).indirect(off))
+        if q is V:
+            return V.tensor_copy(T[dst + "s"][:, a:b], T[src + "s"][:, 0:n].indirect(off))
+        return A.activation(T[dst + "s"][:, a:b], T[src + "s"][:, 0:n].indirect(off), Copy)
 
-    def send_a(call, codes, more=()):
-        snd, win = (T.sndw, T.win) if codes else (T.sndws, T.wins)
-        send(call, lambda d: win[:, spare:spare + CW] if d in near else snd[:, CW * d:CW * d + CW],
-             lambda d: win[:, slot(me, d):slot(me, d) + CW], codes, "arwc" if codes else "arws", more)
+    picked = {}
 
-    wait(g, "pka1")
-    send_a(plan["arwc"][0], True)
-    wait(g, "pka0")
-    send_a(plan["arwc"][1], True)
-    wait(g, "pkas1")
-    send_a([], False, [(c, e, T.sndws[:, CW * d:CW * d + CW], T.hws[:, 0:CW], S.hopa)
-                       for (c, e), d in zip(_deal(_helpers(T, topo, me), inn[:H * HOPA]), two)])
-    wait(g, "pka2")
-    send_a(plan["arwc"][2], True)
-    wait(g, "pkas0", "pkas2")
-    send_a(plan["arws"][0], False)
+    def pick(q, kind, run):
+        a, b = run
+        if kind[0] == "p":
+            call = gather(q, kind == "pc", "land" if run == _run(kind, [me]) else "sndp", a, b, "win", WIN, T.offb[:, a // 16:b // 16])
+        else:
+            dst, at = ("win", _slot(T, topo, me, me) if me == pair[0] else spare) if run == _run(kind, pair) else ("sndw", a)
+            call = gather(q, kind == "wc", dst, at, at + b - a, "nwq", NW, T.offa[:, a // 16:b // 16])
+        picked[kind, run] = "pk%d" % len(picked)
+        call.then_inc(S[picked[kind, run]], 1)
+
+    left, seen = [0], set()
+
+    def send(plan):
+        for call in plan:
+            ts = []
+            for t in call:
+                kind, run, via, e = t
+                for sem in [v for (k, (a, b)), v in picked.items() if k == kind and a < run[1] and run[0] < b and v not in seen]:
+                    seen.add(sem)
+                    wait(g, sem)
+                src = _view(T, kind, ("win", ""), spare, run) if run == _run("w", [near]) else _view(T, kind, ("sndw", "sndp"), run[0], run)
+                if via is None:
+                    ts.append((e, src) + _landing(T, topo, me, kind, run))
+                else:
+                    j = _jobs(T, topo, me, via).index(t)
+                    ts.append((e, src, _helpers(T, topo, me)[via], _view(T, kind, ("hw", "hp"), 2 * PC * j, run), S["hop%d" % j]))
+            left[0] += _fused(g, T, topo, ts)
+
+    wait(V, z, ("dnw", 16))
+    V.quantize_mx(T.nwq[:, :], T.nwqs[:, :], T.nwt[:, :]).then_inc(S.nq, 1)
+    wait(V, ("dwr", 64))
+    for k in range(2):
+        V.tensor_copy(T.offa[64 * k:64 * k + 64, :], T.lwr[0:64, :]).then_inc(S.oa, 1)
+    for q, kind, chips in ((V, "wc", away + [pair]), (A, "ws", away[1:] + away[:1] + [pair])):
+        wait(q, "nq", ("oa", 2))
+        for m in chips:
+            pick(q, kind, _run(kind, m))
+    send(plan_a)
 
     def pool(k):
-        a, b = CUTS[k], CUTS[k + 1]
+        a, b = CC * k, CC * k + CC
         wait(V, ("dpl%d" % k, 16))
         V.quantize_mx(T.win[:, NEW + a:NEW + b], T.wins[:, NEW + a:NEW + b], T.plt[:, 4 * a:4 * b]).then_inc(S["plq%d" % k], 1)
 
+    wait(V, ("dwp", 64), "i_s", a3)
+    for p in quads:
+        V.tensor_scalar(T.w1[p, :], T.lwp[0:32, :], 1023, None, Op.bitwise_and).then_inc(S.rep, 1)
     pool(0)
-    wait(V, b1)
-    b2 = step(V.tensor_tensor(T.w2[:, :], T.w1[:, :], T.cslot[:, 0:8], Op.min))
+    wait(V, ("rep", 4))
+    b2 = step(V.tensor_tensor(T.w2[:, :], T.w1[:, 0:8], T.cslot[:, 0:8], Op.min))
+    wait(V, a4)
+    c1 = step(V.tensor_scalar(T.offr[:, 0:3], T.w1[:, 8:11], float(PG - 1), T.colq[:, 0:1], Op.min, Op.add))
     wait(V, b2)
     b3 = step(V.tensor_scalar(T.offw[:, :], T.w2[:, :], T.cold[:, 0:1], None, Op.add))
     wait(V, b3, row, ("i_k", 2))
@@ -267,82 +293,63 @@ def rank_program(g, core, T, topo):
     pool(1)
     wait(V, b4)
     b5 = step(V.transpose(T.srct[:, :], T.srow[:, 0:ROW]))
-    wait(V, ("drd", 128), a4)
-    c1 = step(V.tensor_scalar(T.offr[:, 0:3], T.lrd[:, 0:3], T.colq[:, 0:1], None, Op.add))
+    pool(2)
     wait(V, b5, "bs")
     b6 = step(V.tensor_tensor(T.srcf[:, :], T.srct[:, 0:ROW:16], T.cbase[:, :], Op.min))
-    pool(2)
+    pool(3)
     wait(V, b6, c1)
     V.tensor_copy(T.offb[:, :], T.srcf[:, :].indirect(T.offr[:, 0:3])).then_inc(S.ob, 1)
+    pooled = ["plq%d" % k for k in range(CH)]
 
     wait(A, "i_s", "cb")
     A.activation(T.cbase[:, :], T.cslot[:, 0:FR], Ident, bias=T.colb[:, 0:1]).then_inc(S.bs, 1)
     wait(A, "cg")
-    A.activation(T.wslot[:, :], T.cslot[:, :], Ident, bias=T.colg[:, 0:1]).then_inc(S.ws, 1)
+    A.activation(T.wslot[:, :], T.cslot[:, :], Ident, bias=T.colg[:, 0:1]).then_inc(S.cw, 1)
 
-    picks = [([d], "sndp") for d in away[0]] + [(away[1], "sndp"), (away[2], "sndp"), (near, "sndp"), ([me], "land")]
-
-    def pick_b(k, q, codes):
-        m, buf = picks[k]
-        a, b, off = PC * m[0], PC * (m[-1] + 1), T.offb[:, CP * m[0]:CP * (m[-1] + 1)]
-        if codes:
-            V.tensor_copy(T[buf][:, a:b].bitcast(dt.uint32), T.win[:, :].bitcast(dt.uint32).indirect(off)).then_inc(S["pkb%d" % k], 1)
-        elif q is V:
-            V.tensor_copy(T[buf + "s"][:, a:b], T.wins[:, :].indirect(off)).then_inc(S["pkbs%d" % k], 1)
-        else:
-            A.activation(T[buf + "s"][:, a:b], T.wins[:, :].indirect(off), Copy).then_inc(S["pkbs%d" % k], 1)
-
-    wait(V, "pka2", "plq0", "plq1", "plq2", "ob", arrive["arwc"])
-    for k in range(len(picks)):
-        pick_b(k, V, True)
-    for q, part in ((A, (0, 1, 3, 5)), (V, (2, 4))):
-        wait(q, "pkas2", "plq0", "plq1", "plq2", "ob", arrive["arws"])
-        for k in part:
-            pick_b(k, q, False)
-    hop = [(c, e, T.sndp[:, PC * d:PC * d + PC], T.hp[:, 0:PC], S.hopb)
-           for (c, e), d in zip(_deal(_helpers(T, topo, me), inn[:H * HOPB]), away[1])]
-    codes, scales = plan["arpc"], plan["arps"]
-    for need, call, more in (((0,), codes[0], ()), ((1,), codes[1], ()), ((2,), [], hop), ((3, 4), codes[2], ())):
-        wait(g, *["pkb%d" % k for k in need])
-        send(call, lambda d: T.sndp[:, PC * d:PC * d + PC], lambda d: T.land[:, PC * me:PC * me + PC], True, "arpc", more)
-    for need, call in (((0, 1, 2), scales[0]), ((3, 4), scales[1])):
-        wait(g, *["pkbs%d" % k for k in need])
-        send(call, lambda d: T.sndps[:, PC * d:PC * d + PC], lambda d: T.lands[:, PC * me:PC * me + PC], False, "arps")
+    wait(V, picked["wc", _run("w", pair)], *pooled, "ob", arrive["wc"])
+    wait(A, picked["ws", _run("w", pair)], *pooled, "ob", arrive["ws"])
+    runs = [t[1] for call in plan_b for t in call if t[0] == "pc"]
+    for i, call in enumerate(plan_b):
+        if call[0][0] == "pc":
+            pick(V, "pc", call[0][1])
+            continue
+        if all(c[0][0] == "pc" for c in plan_b[:i]):
+            wait(V, picked["ws", _run("w", pair)], arrive["ws"])
+        for q, run in zip((A, V), [x for x in runs if call[0][1][0] <= x[0] < call[-1][1][1]]):
+            pick(q, "ps", run)
+    pick(A, "ps", _run("p", [me]))
+    pick(V, "pc", _run("p", [me]))
+    send(plan_b)
     g.wait_ge(S.left, left[0])
 
-    wait(V, ("dpg", 128))
-    e2 = step(V.tensor_copy(T.offg[:, :], T.lpg[:, :]))
-    wait(V, e2, "ws")
-    V.tensor_copy(T.offc[:, :], T.wslot[:, :].indirect(T.offg[:, 0:2])).then_inc(S.oc, 1)
+    wait(V, ("dpg", 32))
+    for p in quads:
+        V.tensor_copy(T.offg[p, :], T.lpg[0:32, :]).then_inc(S.og, 1)
     wait(V, ("dqw", 16))
     V.quantize_mx(T.qwq[:, :], T.qws[:, :], T.qwt[:, :]).then_inc(S.qwd, 1)
+    wait(V, ("og", 4), "cw")
+    V.tensor_copy(T.offc[:, :], T.wslot[:, :].indirect(T.offg[:, 0:2])).then_inc(S.oc, 1)
 
-    k = CC // 16
-    wait(V, "pkb5", "oc", arrive["arpc"])
-    for c in range(CH):
-        V.tensor_copy(T.fin[:, CC * c:CC * c + CC].bitcast(dt.uint32),
-                      T.land[:, :].bitcast(dt.uint32).indirect(T.offc[:, k * c:k * c + k])).then_inc(S["fc%d" % c], 1)
-    wait(A, "pkbs5", "oc", arrive["arps"])
-    for c in range(CH):
-        A.activation(T.fins[:, CC * c:CC * c + CC], T.lands[:, :].indirect(T.offc[:, k * c:k * c + k]), Copy).then_inc(S["fs%d" % c], 1)
+    order = [(c, (c + o + 1) % O) for c in range(CH) for o in range(O)]
+    stores = [order[:1]] + [order[k:k + 2] for k in range(1, len(order), 2)]
+    for q, kind, mine in ((V, "pc", order[0::2]), (A, "ps", order[1::2])):
+        wait(q, picked[kind, _run("p", [me])], "oc", arrive[kind])
+        for c in range(CH):
+            a, b = CC * c, CC * c + CC
+            gather(q, q is V, "fin", a, b, "land", N * PC, T.offc[:, a // 16:b // 16]).then_inc(S["f%s%d" % (kind[1], c)], 1)
+        for c, o in mine:
+            wait(q, "mm%d" % (O * c + o))
+            y, v = T.yb[:, 512 * o + CC * c:512 * o + CC * c + CC], T.ps[:, 512 * (O * c + o):512 * (O * c + o) + CC]
+            (A.activation(y, v, Copy) if q is A else V.tensor_copy(y, v)).then_inc(S["cp%d" % (O * c + o)], 1)
     wait(P, "qwd")
-    stores = [(1, (0,)), (0, (0, 1)), (1, (1, 2)), (0, (2, 3)), (1, (3,))]
-    ready = []
-    for o, c in [(o, c) for o, cs in stores for c in cs]:
-        if c not in ready:
-            ready.append(c)
+    for c, o in order:
+        if (c, o) in order[0::2]:
             wait(P, "fc%d" % c, "fs%d" % c)
-        b = O * c + o
-        P.matmul_mx(T.ps[:, 512 * b:512 * b + CC], T.qwq[:, 128 * o:128 * o + 128], T.qws[:, 128 * o:128 * o + 128],
-                    T.fin[:, CC * c:CC * c + CC], T.fins[:, CC * c:CC * c + CC], True, True).then_inc(S["mm%d" % b], 1)
-    for o, cs in stores:
-        for c in cs:
-            b, at = O * c + o, 512 * o + CC * c
-            q = A if (o, c) == (1, 3) else V
-            wait(q, "mm%d" % b)
-            a, v = T.yb[:, at:at + CC], T.ps[:, 512 * b:512 * b + CC]
-            (A.activation(a, v, Copy) if q is A else V.tensor_copy(a, v)).then_inc(S["cp%d" % b], 1)
-            wait(Y, "cp%d" % b)
-        a, b = 512 * o + CC * cs[0], 512 * o + CC * (cs[-1] + 1)
+        a, b, k = CC * c, CC * c + CC, O * c + o
+        P.matmul_mx(T.ps[:, 512 * k:512 * k + CC], T.qwq[:, 128 * o:128 * o + 128], T.qws[:, 128 * o:128 * o + 128],
+                    T.fin[:, a:b], T.fins[:, a:b], True, True).then_inc(S["mm%d" % k], 1)
+    for part in stores:
+        wait(Y, *["cp%d" % (O * c + o) for c, o in part])
+        a, b = 512 * part[0][1] + CC * part[0][0], 512 * part[0][1] + CC * (part[-1][0] + 1)
         Y.dma_start(T.y[:, a:b], T.yb[:, a:b]).then_inc(S.ystore, 16)
     Y.wait_ge(S.ystore, 16 * len(stores))

from concourse.bass import DstId, RemoteDMATransfer
from concourse.mybir import dt, AluOpType, ActivationFunctionType

N = 8
PG, NW, SP, CW, CP, O = 32, 64, 32, 16, 6, 2
POOL = 16 * PG
SLOTS = N * CW
NEW = SLOTS + CW
WIN = NEW + POOL
PC = 16 * CP
ROW = POOL + 32
FR = ROW // 16
DUMP = ROW - 16
SROW = 800
NONE = 1024.0
CH = 4
CC = POOL // CH
H = 2
JOBS = 3
LENT = 32

F8, U8, U16, I32, F32, BF = "float8_e4m3fn_x4", "uint8", "uint16", "int32", "float32", "bfloat16"


def _sb(n, d):
    return ("sbuf", [128, n], d)


SCRATCH = {
    "nwt": _sb(512, BF), "plt": _sb(4 * POOL, BF), "qwt": _sb(512 * O, BF),
    "lwr": _sb(8, I32), "lwp": _sb(11, I32), "lpg": _sb(2, I32),
    "pcol": _sb(1, I32), "pand": _sb(3, I32), "cold": _sb(1, F32), "colq": _sb(1, F32), "colg": _sb(1, F32),
    "colb": _sb(1, F32), "kval": _sb(SLOTS, BF), "cslot": _sb(48, F32), "wslot": _sb(48, F32), "cbase": _sb(FR, F32),
    "offa": _sb(8, U16), "offw": _sb(8, U16), "offr": _sb(4, U16),
    "offb": _sb(48, U16), "offg": _sb(2, U16), "offc": _sb(32, U16),
    "w1": _sb(11, I32), "w2": _sb(8, F32), "srcf": _sb(FR, F32),
    "srow": _sb(SROW, BF), "srct": _sb(ROW, BF),
    "nwq": _sb(128, F8), "nwqs": _sb(128, U8),
    "sndw": _sb(SLOTS, F8), "sndws": _sb(SLOTS, U8),
    "win": _sb(WIN, F8), "wins": _sb(WIN, U8),
    "sndp": _sb(N * PC, F8), "sndps": _sb(N * PC, U8),
    "land": _sb(N * PC, F8), "lands": _sb(N * PC, U8),
    "hws": _sb(2 * CW, U8), "hp": _sb(JOBS * 2 * PC, F8),
    "fin": _sb(16 * SP, F8), "fins": _sb(16 * SP, U8),
    "qwq": _sb(128 * O, F8), "qws": _sb(128 * O, U8),
    "ps": ("psum", [128, 512 * CH * O], F32),
    "yb": _sb(512 * O, F32),
}
KINDS = ("wc", "ws", "pc", "ps")
WIDE = {"w": CW, "p": PC}
SEMAPHORES = (["dnw", "dwr", "dwp", "dpg", "dqw", "ystore"] + ["dpl%d" % k for k in range(CH)] + ["plq%d" % k for k in range(CH)]
              + ["i_p", "i_k", "i_s", "cg", "cb", "cw", "bs", "rep", "og", "nq", "oa", "oc", "ob", "qwd"]
              + ["v%d" % k for k in range(16)] + ["pk%d" % k for k in range(3 * N)]
              + ["fc%d" % k for k in range(CH)] + ["fs%d" % k for k in range(CH)]
              + ["mm%d" % k for k in range(CH * O)] + ["cp%d" % k for k in range(CH * O)]
              + ["ar" + k for k in KINDS] + ["left"] + ["hop%d" % k for k in range(JOBS)])


def _chips(T, topo):
    chips = {}
    for r, c in enumerate(T.cores):
        chips.setdefault(topo.chip(c), []).append(r)
    return [chips[k] for k in sorted(chips)]


def _roads(T, topo, r):
    chips = _chips(T, topo)
    at = [k for k, m in enumerate(chips) if r in m][0]
    away = [chips[(at + k) % len(chips)] for k in range(1, len(chips))]
    near = [q for q in chips[at] if q != r][0]
    out = topo.engines(T.cores[r], T.cores[away[0][0]])
    inn = [e for e in topo.engines(T.cores[r], T.cores[near]) if e not in out]
    return away, near, out, inn


def _run(kind, m):
    return WIDE[kind[0]] * m[0], WIDE[kind[0]] * (m[-1] + 1)


def _parts(kind, run):
    w = WIDE[kind[0]]
    parts = [(max(run[0], w * d), min(run[1], w * d + w)) for d in range(run[0] // w, (run[1] - 1) // w + 1)]
    return sorted(parts, key=lambda p: p[0] - p[1])


def _deal(kind, runs, engines, via=None):
    k = len(engines) // len(runs)
    return [(kind, run, via, engines[k * i:k * i + k]) for i, run in enumerate(runs)]


def _plan(T, topo, r):
    away, near, out, inn = _roads(T, topo, r)
    own = [[d for d in m if topo.die(T.cores[d]) == topo.die(T.cores[r])][0] for m in away]
    far = [[d for d in m if d not in own][0] for m in away]

    def each(kind, ds, engines, via=None):
        return _deal(kind, [_run(kind, [d]) for d in ds], engines, via)

    a = [each("wc", far[:1], out), each("wc", away[1] + away[2], out),
         _deal("ws", [_run("ws", away[1])], inn, 0), each("ws", far[2:], inn, 1),
         each("wc", [near], inn) + each("wc", own[:1], out),
         each("ws", own[2:], out) + each("ws", [near], inn)] + [each("ws", [d], out) for d in away[0]]
    lo, hi = _run("pc", away[0])
    kept, lent = ((lo, lo + PC - LENT), (lo + PC - LENT, hi)) if far[0] < own[0] else ((hi - PC + LENT, hi), (lo, hi - PC + LENT))
    scales = [each("ps", m, out) for m in away]
    b = [_deal("pc", [kept], out), _deal("pc", [lent], inn, 0), each("pc", far[1:2], out), each("pc", own[1:2], inn, 1),
         each("pc", own[2:], inn, 0), each("pc", far[2:], out),
         scales[1], each("pc", [near], inn), scales[2], scales[0], each("ps", [near], inn)]
    return a, b


def _helpers(T, topo, r):
    c = T.cores[r]
    return [k for k in topo.cores_of(c) if topo.die(k) == topo.die(c) and T.rank_of(k) is None][:H]


def _jobs(T, topo, r, h):
    return [t for call in sum(_plan(T, topo, r), []) for t in call if t[2] == h]


def _onward(T, topo, r, job):
    out, parts = _roads(T, topo, r)[2], _parts(*job[:2])
    if len({b - a for a, b in parts}) == 1:
        return [_deal(job[0], parts, out)]
    return [_deal(job[0], [p], out) for p in parts]


def _slot(T, topo, s, q):
    first = [m[0] for m in _chips(T, topo) if q in m][0]
    return CW * (s + (s > first))


def _view(T, kind, names, at, run):
    v = T[names[kind[0] == "p"] + ("s" if kind[1] == "s" else "")][:, at:at + run[1] - run[0]]
    return v.bitcast(dt.uint8) if kind[1] == "c" else v


def _landing(T, topo, s, kind, run):
    q, at = divmod(run[0], WIDE[kind[0]])
    return T.cores[q], _view(T, kind, ("win", "land"), at + (PC * s if kind[0] == "p" else _slot(T, topo, s, q)), run), T.sem["ar" + kind]


def _fused(g, T, topo, ts):
    out = []
    for engines, a, c, b, sem in ts:
        rid, pid, _ = topo.addr(c)
        out.append(RemoteDMATransfer(dst_ids=[DstId(rid=rid, pnc=pid)], dma_engine_mask=sum(1 << e for e in engines),
                                     remote_sem=sem, src=a, dst=b))
    g.remote_dma_fused(out, local_sem=T.sem.left)
    return sum(len(t[0]) for t in ts)


def helper_program(g, r, h, T, topo):
    n = 0
    for j, job in enumerate(_jobs(T, topo, r, h)):
        g.wait_ge(T.sem["hop%d" % j], len(job[3]))
        for call in _onward(T, topo, r, job):
            n += _fused(g, T, topo, [(e, _view(T, kind, ("hw", "hp"), 2 * PC * j + run[0] - job[1][0], run)) + _landing(T, topo, r, kind, run)
                                     for kind, run, _, e in call])
    g.wait_ge(T.sem.left, n)


def rank_program(g, core, T, topo):
    me = T.rank_of(core)
    if me is None:
        for r in range(N):
            if core in _helpers(T, topo, r):
                helper_program(g, r, _helpers(T, topo, r).index(core), T, topo)
        return
    S = T.sem
    V, A, P, Y = g.vector, g.scalar, g.tensor, g.sync
    Op, Copy, Ident = AluOpType, ActivationFunctionType.Copy, ActivationFunctionType.Identity
    nv = [0]

    def wait(q, *evs):
        for e in evs:
            n, k = e if isinstance(e, tuple) else (e, 1)
            q.wait_ge(S[n], k)

    def step(call):
        n = "v%d" % nv[0]
        nv[0] += 1
        call.then_inc(S[n], 1)
        return n

    away, near, out, inn = _roads(T, topo, me)
    plan_a, plan_b = _plan(T, topo, me)
    arrive = {kind: 0 for kind in KINDS}
    for r in range(N):
        for t in [t for call in sum(_plan(T, topo, r), []) for t in call]:
            for kind, run, _, e in [t] if t[2] is None else sum(_onward(T, topo, r, t), []):
                arrive[kind] += len(e) * (run[0] // WIDE[kind[0]] == me)
    arrive = {kind: ("ar" + kind, n) for kind, n in arrive.items()}
    pair = sorted([me, near])
    spare = CW * pair[1]
    quads = [slice(32 * k, 32 * k + 32) for k in range(4)]

    def table(q, dst, src, at, cols, sem, groups):
        for k in groups:
            q.dma_start(dst[16 * k:16 * k + 16, at:at + cols], src[:, :]).then_inc(S[sem], 16)

    table(A, T.lwr, T.wr, 0, 8, "dwr", [0, 1])
    table(A, T.lwp, T.wp, 0, 8, "dwp", [0, 1])
    table(A, T.lwp, T.rd, 8, 3, "dwp", [0])
    Y.dma_start(T.nwt[:, 0:4 * NW], T.nw[:, :]).then_inc(S.dnw, 16)
    table(Y, T.lwr, T.wr, 0, 8, "dwr", [2, 3])
    for k in range(CH):
        Y.dma_start(T.plt[:, 4 * CC * k:4 * CC * (k + 1)], T.pl[:, 4 * CC * k:4 * CC * (k + 1)]).then_inc(S["dpl%d" % k], 16)
        if k == 0:
            table(Y, T.lwp, T.rd, 8, 3, "dwp", [1])
    Y.dma_start(T.qwt[:, :], T.qw[:, :]).then_inc(S.dqw, 16)
    table(Y, T.lpg, T.pg, 0, 2, "dpg", [0, 1])

    g.iota(T.pcol[:, :], [[1, 1]], 0, 1).then_inc(S.i_p, 1)
    g.iota(T.cslot[:, :], [[16, 48]], DUMP, 1, allow_small_or_imprecise_dtypes=True).then_inc(S.i_s, 1)
    g.iota(T.kval[:, 0:spare], [[1, spare]], 0, 0, allow_small_or_imprecise_dtypes=True).then_inc(S.i_k, 1)
    g.iota(T.kval[:, spare:SLOTS], [[1, SLOTS - spare]], spare + CW, 0, allow_small_or_imprecise_dtypes=True).then_inc(S.i_k, 1)
    row = step(V.memset(T.srow[:, 0:ROW], NONE))
    wait(V, "i_p")
    bits = [step(V.tensor_scalar(T.pand[:, k:k + 1], T.pcol[:, 0:1], m, None, Op.bitwise_and)) for k, m in enumerate((16, 112, 96))]
    z = step(V.memset(T.nwt[:, 4 * NW:512], 0.0))
    wait(V, *bits)
    a3 = step(V.tensor_scalar(T.cold[:, :], T.pand[:, 0:1], -1.0, 32.0, Op.mult, Op.add))
    a4 = step(V.tensor_scalar(T.colq[:, :], T.pand[:, 0:1], -1.0 / 16, 2.0, Op.mult, Op.add))
    V.tensor_scalar(T.colg[:, :], T.pand[:, 1:2], -1.0, -float(DUMP), Op.mult, Op.add).then_inc(S.cg, 1)
    V.tensor_scalar(T.colb[:, :], T.pand[:, 2:3], -1.0, float(NEW - DUMP - 32), Op.mult, Op.add).then_inc(S.cb, 1)

    def gather(q, codes, dst, a, b, src, n, off):
        if codes:
            return V.tensor_copy(T[dst][:, a:b].bitcast(dt.uint32), T[src][:, 0:n].bitcast(dt.uint32).indirect(off))
        if q is V:
            return V.tensor_copy(T[dst + "s"][:, a:b], T[src + "s"][:, 0:n].indirect(off))
        return A.activation(T[dst + "s"][:, a:b], T[src + "s"][:, 0:n].indirect(off), Copy)

    picked = {}

    def pick(q, kind, run):
        a, b = run
        if kind[0] == "p":
            call = gather(q, kind == "pc", "land" if run == _run(kind, [me]) else "sndp", a, b, "win", WIN, T.offb[:, a // 16:b // 16])
        else:
            dst, at = ("win", _slot(T, topo, me, me) if me == pair[0] else spare) if run == _run(kind, pair) else ("sndw", a)
            call = gather(q, kind == "wc", dst, at, at + b - a, "nwq", NW, T.offa[:, a // 16:b // 16])
        picked[kind, run] = "pk%d" % len(picked)
        call.then_inc(S[picked[kind, run]], 1)

    left, seen = [0], set()

    def send(plan):
        for call in plan:
            ts = []
            for t in call:
                kind, run, via, e = t
                for sem in [v for (k, (a, b)), v in picked.items() if k == kind and a < run[1] and run[0] < b and v not in seen]:
                    seen.add(sem)
                    wait(g, sem)
                src = _view(T, kind, ("win", ""), spare, run) if run == _run("w", [near]) else _view(T, kind, ("sndw", "sndp"), run[0], run)
                if via is None:
                    ts.append((e, src) + _landing(T, topo, me, kind, run))
                else:
                    j = _jobs(T, topo, me, via).index(t)
                    ts.append((e, src, _helpers(T, topo, me)[via], _view(T, kind, ("hw", "hp"), 2 * PC * j, run), S["hop%d" % j]))
            left[0] += _fused(g, T, topo, ts)

    wait(V, z, ("dnw", 16))
    V.quantize_mx(T.nwq[:, :], T.nwqs[:, :], T.nwt[:, :]).then_inc(S.nq, 1)
    wait(V, ("dwr", 64))
    for k in range(2):
        V.tensor_copy(T.offa[64 * k:64 * k + 64, :], T.lwr[0:64, :]).then_inc(S.oa, 1)
    for q, kind, chips in ((V, "wc", away + [pair]), (A, "ws", away[1:] + away[:1] + [pair])):
        wait(q, "nq", ("oa", 2))
        for m in chips:
            pick(q, kind, _run(kind, m))
    send(plan_a)

    def pool(k):
        a, b = CC * k, CC * k + CC
        wait(V, ("dpl%d" % k, 16))
        V.quantize_mx(T.win[:, NEW + a:NEW + b], T.wins[:, NEW + a:NEW + b], T.plt[:, 4 * a:4 * b]).then_inc(S["plq%d" % k], 1)

    wait(V, ("dwp", 64), "i_s", a3)
    for p in quads:
        V.tensor_scalar(T.w1[p, :], T.lwp[0:32, :], 1023, None, Op.bitwise_and).then_inc(S.rep, 1)
    pool(0)
    wait(V, ("rep", 4))
    b2 = step(V.tensor_tensor(T.w2[:, :], T.w1[:, 0:8], T.cslot[:, 0:8], Op.min))
    wait(V, a4)
    c1 = step(V.tensor_scalar(T.offr[:, 0:3], T.w1[:, 8:11], float(PG - 1), T.colq[:, 0:1], Op.min, Op.add))
    wait(V, b2)
    b3 = step(V.tensor_scalar(T.offw[:, :], T.w2[:, :], T.cold[:, 0:1], None, Op.add))
    wait(V, b3, row, ("i_k", 2))
    b4 = step(V.tensor_copy(T.srow[:, :].indirect(T.offw[:, :]), T.kval[:, :]))
    pool(1)
    wait(V, b4)
    b5 = step(V.transpose(T.srct[:, :], T.srow[:, 0:ROW]))
    pool(2)
    wait(V, b5, "bs")
    b6 = step(V.tensor_tensor(T.srcf[:, :], T.srct[:, 0:ROW:16], T.cbase[:, :], Op.min))
    pool(3)
    wait(V, b6, c1)
    V.tensor_copy(T.offb[:, :], T.srcf[:, :].indirect(T.offr[:, 0:3])).then_inc(S.ob, 1)
    pooled = ["plq%d" % k for k in range(CH)]

    wait(A, "i_s", "cb")
    A.activation(T.cbase[:, :], T.cslot[:, 0:FR], Ident, bias=T.colb[:, 0:1]).then_inc(S.bs, 1)
    wait(A, "cg")
    A.activation(T.wslot[:, :], T.cslot[:, :], Ident, bias=T.colg[:, 0:1]).then_inc(S.cw, 1)

    wait(V, picked["wc", _run("w", pair)], *pooled, "ob", arrive["wc"])
    wait(A, picked["ws", _run("w", pair)], *pooled, "ob", arrive["ws"])
    runs = [t[1] for call in plan_b for t in call if t[0] == "pc"]
    for i, call in enumerate(plan_b):
        if call[0][0] == "pc":
            pick(V, "pc", call[0][1])
            continue
        if all(c[0][0] == "pc" for c in plan_b[:i]):
            wait(V, picked["ws", _run("w", pair)], arrive["ws"])
        for q, run in zip((A, V), [x for x in runs if call[0][1][0] <= x[0] < call[-1][1][1]]):
            pick(q, "ps", run)
    pick(A, "ps", _run("p", [me]))
    pick(V, "pc", _run("p", [me]))
    send(plan_b)
    g.wait_ge(S.left, left[0])

    wait(V, ("dpg", 32))
    for p in quads:
        V.tensor_copy(T.offg[p, :], T.lpg[0:32, :]).then_inc(S.og, 1)
    wait(V, ("dqw", 16))
    V.quantize_mx(T.qwq[:, :], T.qws[:, :], T.qwt[:, :]).then_inc(S.qwd, 1)
    wait(V, ("og", 4), "cw")
    V.tensor_copy(T.offc[:, :], T.wslot[:, :].indirect(T.offg[:, 0:2])).then_inc(S.oc, 1)

    order = [(c, (c + o + 1) % O) for c in range(CH) for o in range(O)]
    stores = [order[:1]] + [order[k:k + 2] for k in range(1, len(order), 2)]
    for q, kind, mine in ((V, "pc", order[0::2]), (A, "ps", order[1::2])):
        wait(q, picked[kind, _run("p", [me])], "oc", arrive[kind])
        for c in range(CH):
            a, b = CC * c, CC * c + CC
            gather(q, q is V, "fin", a, b, "land", N * PC, T.offc[:, a // 16:b // 16]).then_inc(S["f%s%d" % (kind[1], c)], 1)
        for c, o in mine:
            wait(q, "mm%d" % (O * c + o))
            y, v = T.yb[:, 512 * o + CC * c:512 * o + CC * c + CC], T.ps[:, 512 * (O * c + o):512 * (O * c + o) + CC]
            (A.activation(y, v, Copy) if q is A else V.tensor_copy(y, v)).then_inc(S["cp%d" % (O * c + o)], 1)
    wait(P, "qwd")
    for c, o in order:
        if (c, o) in order[0::2]:
            wait(P, "fc%d" % c, "fs%d" % c)
        a, b, k = CC * c, CC * c + CC, O * c + o
        P.matmul_mx(T.ps[:, 512 * k:512 * k + CC], T.qwq[:, 128 * o:128 * o + 128], T.qws[:, 128 * o:128 * o + 128],
                    T.fin[:, a:b], T.fins[:, a:b], True, True).then_inc(S["mm%d" % k], 1)
    for part in stores:
        wait(Y, *["cp%d" % (O * c + o) for c, o in part])
        a, b = 512 * part[0][1] + CC * part[0][0], 512 * part[0][1] + CC * (part[-1][0] + 1)
        Y.dma_start(T.y[:, a:b], T.yb[:, a:b]).then_inc(S.ystore, 16)
    Y.wait_ge(S.ystore, 16 * len(stores))
